import numpy as np
import ml_dtypes


def mxq(x, axis, fmt="e4m3"):
    dtype, down = {"e4m3": (ml_dtypes.float8_e4m3fn, 7), "e5m2": (ml_dtypes.float8_e5m2, 14)}[fmt]
    v = np.moveaxis(np.asarray(x, np.float32).astype(ml_dtypes.bfloat16).astype(np.float64), axis, -1)
    blocks = v.reshape(v.shape[:-1] + (-1, 32))
    amax = np.abs(blocks).max(-1, keepdims=True)
    byte = np.maximum(np.where(amax > 0, np.frexp(amax)[1] - 1 + 127, 0) - down, 1)
    scale = np.exp2(byte - 127.0)
    codes = (blocks / scale).astype(np.float32).astype(dtype).astype(np.float64)
    return np.moveaxis((codes * scale).reshape(v.shape), -1, axis)


WIDE = False


def mx_kscale(k):
    if not WIDE:
        return np.ones(k)
    levels = np.array([10, -10, 5, -5, 0])
    if k % 512:
        return np.exp2(np.random.permutation(np.resize(levels, k // 32))).repeat(32)
    a = np.empty((k // 512, 16))
    for p in range(k // 512):
        a[p, :8] = np.random.permutation(np.resize(levels, 8))
        for g in range(8):
            far = levels[np.abs(levels - a[p, g]) >= 10]
            a[p, g + 8] = far[np.random.randint(len(far))]
    return np.exp2(a.ravel()).repeat(32)


def f64(x):
    return np.asarray(x).astype(np.float64)


def striped8(idx):
    return np.concatenate([x.reshape(-1, 16).T for x in idx]).astype(np.uint16)


def runs(offs, k):
    lists = np.stack([offs[16 * r : 16 * r + 16].T.reshape(-1) for r in range(8)]).astype(np.int64)
    return lists[np.arange(k) % 512 // 64]


def pack_weight(w):
    k, n = w.shape
    w = f64(np.asarray(w, np.float32).astype(ml_dtypes.bfloat16)).reshape(k // 32, 32, n)
    amax = np.abs(w).max(1)
    byte = np.clip(np.where(amax > 0, np.frexp(amax)[1] - 1 + 127 - 7, 1), 1, 254)
    scaled = (w * np.exp2(127.0 - byte)[:, None, :]).reshape(k, n).astype(np.float32)
    words = np.ascontiguousarray(scaled.reshape(k // 512, 128, 4, n).transpose(0, 1, 3, 2)).astype(ml_dtypes.float8_e4m3fn).view(np.uint8)
    return words, np.ascontiguousarray(byte.astype(np.uint8).reshape(k // 512, 16, n))


def unpack_weight(words, scales):
    g, p, n, _ = words.shape
    vals = np.ascontiguousarray(words).view(ml_dtypes.float8_e4m3fn).astype(np.float64) * np.repeat(np.exp2(scales.astype(np.float64) - 127.0), 8, axis=1)[..., None]
    return vals.transpose(0, 1, 3, 2).reshape(g * 512, n)


def relu(v):
    return np.maximum(v, 0.0)


K, T, S, H, N = 1024, 2048, 1024, 512, 128


def setup_inputs():
    n = np.random.standard_normal
    s = mx_kscale(K)[:, None]
    u = mx_kscale(H)
    packed_xT = pack_weight(n((K, T)) * s)
    packed_w2 = pack_weight(n((H, N)) / np.sqrt(H) / u[:, None])
    return {
        "x_words": packed_xT[0],
        "x_scales": packed_xT[1],
        "w1": (n((K, H)) / np.sqrt(K) / s * u).astype(np.float32),
        "w2_words": packed_w2[0],
        "w2_scales": packed_w2[1],
        "pos": (0.5 * n((H, S)) * u[:, None]).astype(np.float32),
        "offs": striped8(np.random.randint(0, T, (8, S))),
    }


def reference(x_words, x_scales, w1, w2_words, w2_scales, pos, offs):
    xq = unpack_weight(x_words, x_scales)[np.arange(K)[:, None], runs(offs, K)]
    h = relu((mxq(f64(w1), 0, "e4m3").T @ xq) + f64(pos))
    return unpack_weight(w2_words, w2_scales).T @ mxq(h, 0, "e4m3")

@@ -1,0 +1,191 @@
+from contextlib import ExitStack
+
+import concourse.mybir as mybir
+
+K, T, S, H, N = 1024, 2048, 1024, 512, 128
+FLOPS = 2 * K * H * S + 2 * H * N * S
+
+F32 = mybir.dt.float32
+BF16 = mybir.dt.bfloat16
+I32 = mybir.dt.int32
+U32 = mybir.dt.uint32
+U16 = mybir.dt.uint16
+U8 = mybir.dt.uint8
+FP8X4 = mybir.dt.float8_e4m3fn_x4
+ADD = mybir.AluOpType.add
+MAX = mybir.AluOpType.max
+COPY = mybir.ActivationFunctionType.Copy
+RELU = mybir.ActivationFunctionType.Relu
+
+P = 128
+PASSES = 2
+BANK = 512
+POS_PIECES = [(0, 256), (256, 512), (512, 768), (768, 1024)]
+CHUNKS = [(0, 256), (256, 512), (512, 768), (768, 896), (896, 1024)]
+OUT_PIECES = [(0, 512), (512, 768), (768, 896), (896, 1024)]
+M_SPLIT = 84
+
+
+def tile_picked_phpq_relu_p_kernel(
+    tc, x_words, x_scales, w1, w2_words, w2_scales, pos, offs, out
+):
+    nc = tc.nc
+    with ExitStack() as ctx:
+        keep = ctx.enter_context(tc.tile_pool(name="keep", bufs=1))
+        psum = ctx.enter_context(tc.psum_pool(name="psum", bufs=1))
+
+        offsets = keep.tile([P, S // 16], U16, name="offsets")
+        nc.sync.dma_start(offsets[:], offs)
+
+        xs_table = keep.tile([P, T], U8, name="xs_table", tag="slot_a", align_bytes=64)
+        nc.gpsimd.memset(xs_table[:].bitcast(I32), 0)
+        nc.scalar.dma_start(
+            xs_table[0:P:4, :].bitcast(I32), x_scales.bitcast(I32).rearrange("z q c -> q z c")
+        )
+
+        def load_x(z, tag):
+            table = keep.tile([P, T], U32, name="xw_table%d" % z, tag=tag, align_bytes=64)
+            nc.sync.dma_start(table[:].bitcast(I32), x_words[z].rearrange("p n t -> p (n t)").bitcast(I32))
+            return table
+
+        def load_w(z, u, raw):
+            rows = w1[512 * z : 512 * (z + 1), 256 * u : 256 * (u + 1)]
+            nc.sync.dma_start(raw, rows.rearrange("(p j) c -> p j c", j=4))
+
+        xw_table0 = load_x(0, "slot_b")
+        w0a = keep.tile([P, 4, 256], F32, name="w0a", align_bytes=64)
+        w0b = keep.tile([P, 4, 256], F32, name="w0b", tag="slot_c", align_bytes=64)
+        load_w(0, 0, w0a[:])
+        load_w(0, 1, w0b[:])
+
+        xs_plane = keep.tile([P, PASSES * S], U8, name="xs_plane", align_bytes=64)
+        nc.vector.memset(xs_plane[:].bitcast(I32), 0)
+        w2_codes = keep.tile([P, N], U32, name="w2_codes", align_bytes=64)
+        w2_plane = keep.tile([P, N], U8, name="w2_plane", align_bytes=64)
+        nc.vector.memset(w2_plane[:].bitcast(I32), 0)
+        nc.gpsimd.dma_start(w2_codes[:].bitcast(I32), w2_words[0].rearrange("p n t -> p (n t)").bitcast(I32))
+        for q in range(4):
+            nc.gpsimd.dma_start(
+                w2_plane[32 * q : 32 * q + 4, :].bitcast(I32), w2_scales[0, 4 * q : 4 * q + 4, :].bitcast(I32)
+            )
+
+        xs_picked = keep.tile([P, S], U8, name="xs_picked", align_bytes=64)
+        nc.vector.tensor_copy(xs_picked[:], xs_table[:].indirect(offsets[:]))
+        for q in range(4):
+            nc.sync.dma_start(
+                xs_plane[32 * q : 32 * q + 4, :].bitcast(I32),
+                xs_picked[32 * q : 32 * q + 32 : 4, :].bitcast(I32),
+            )
+        xw_table1 = load_x(1, "slot_a")
+
+        def gather_words(z, table):
+            picked = keep.tile([P, S], U32, name="xw_picked%d" % z, align_bytes=64)
+            nc.vector.tensor_copy(picked[:], table[:].indirect(offsets[:]))
+            return picked
+
+        xw_picked = [gather_words(0, xw_table0)]
+        w1ab = keep.tile([P, 2, 4, 256], F32, name="w1ab", tag="slot_b", align_bytes=64)
+        load_w(1, 0, w1ab[:, 0])
+        load_w(1, 1, w1ab[:, 1])
+
+        grouped = [keep.tile([P, 4, 128, 4], BF16, name="w_grouped%d" % z, align_bytes=64) for z in range(PASSES)]
+        w_codes = [keep.tile([P, H], U32, name="w_codes%d" % z, align_bytes=64) for z in range(PASSES)]
+        w_plane = [keep.tile([P, H], U8, name="w_plane%d" % z, align_bytes=64) for z in range(PASSES)]
+
+        def cast_views(z, raw, base, m0, m1):
+            dst = grouped[z][:, :, m0:m1, :].rearrange("p t m j -> p m j t")
+            src = raw[:, :, 4 * (m0 - base) : 4 * (m1 - base)].rearrange("p j (m t) -> p m j t", t=4)
+            return dst, src
+
+        def quantise_w(z, t0, t1):
+            cols = slice(128 * t0, 128 * t1)
+            nc.vector.quantize_mx(
+                out=w_codes[z][:, cols].bitcast(FP8X4),
+                scales=w_plane[z][:, cols],
+                in_=grouped[z][:, t0:t1].rearrange("p t m j -> p (t m j)"),
+            )
+
+        nc.scalar.activation(*cast_views(0, w0a[:], 0, 0, 64), COPY)
+        nc.scalar.activation(*cast_views(0, w0b[:], 64, 64, 128), COPY)
+        quantise_w(0, 0, 4)
+
+        pos_view = pos.rearrange("(p t) j -> p t j", t=4)
+        pos_sb = keep.tile([P, 4, S], F32, name="pos_sb", tag="slot_c", align_bytes=64)
+        for a, b in POS_PIECES:
+            nc.sync.dma_start(pos_sb[:, :, a:b], pos_view[:, :, a:b])
+
+        banks = [[psum.tile([P, BANK], F32, name="h_bank", tag="bank%d%d" % (g, t)) for t in range(4)] for g in range(2)]
+
+        def first_layer(z):
+            for g in range(2):
+                for t in range(4):
+                    m_cols = slice(128 * t, 128 * (t + 1))
+                    nc.tensor.matmul_mx(
+                        out=banks[g][t][:],
+                        lhsT=w_codes[z][:, m_cols].bitcast(FP8X4),
+                        lhsT_scale=w_plane[z][:, m_cols],
+                        rhs=xw_picked[z][:, g * BANK : (g + 1) * BANK].bitcast(FP8X4),
+                        rhs_scale=xs_plane[:, z * S + g * BANK : z * S + (g + 1) * BANK],
+                        start=(z == 0),
+                        stop=(z == PASSES - 1),
+                    )
+
+        first_layer(0)
+        xw_picked.append(gather_words(1, xw_table1))
+        nc.scalar.activation(*cast_views(1, w1ab[:, 0], 0, 0, 64), COPY)
+        nc.scalar.activation(*cast_views(1, w1ab[:, 1], 64, 64, M_SPLIT), COPY)
+        nc.vector.tensor_copy(*cast_views(1, w1ab[:, 1], 64, M_SPLIT, 128))
+        for t in range(4):
+            quantise_w(1, t, t + 1)
+        first_layer(1)
+
+        h_codes = keep.tile([P, S], U32, name="h_codes", align_bytes=64)
+        h_plane = keep.tile([P, S], U8, name="h_plane", align_bytes=64)
+
+        def add_and_relu(a, b):
+            g = a // BANK
+            summed = keep.tile([P, 4, b - a], F32, name="summed%d" % a, align_bytes=64)
+            for t in range(4):
+                nc.vector.tensor_tensor(
+                    summed[:, t, :], banks[g][t][:, a - g * BANK : b - g * BANK], pos_sb[:, t, a:b], ADD
+                )
+            h_bf = keep.tile([P, b - a, 4], BF16, name="h_bf%d" % a, align_bytes=64)
+            dst = h_bf[:].rearrange("p (c i) t -> p c t i", i=4)
+            src = summed[:].rearrange("p t (c i) -> p c t i", i=4)
+            if b == S:
+                nc.vector.tensor_scalar_max(dst, src, 0.0)
+            else:
+                nc.scalar.activation(dst, src, RELU)
+            return h_bf
+
+        def quantise_h(a, b, h_bf):
+            nc.vector.quantize_mx(
+                out=h_codes[:, a:b].bitcast(FP8X4), scales=h_plane[:, a:b], in_=h_bf[:].rearrange("p n t -> p (n t)")
+            )
+
+        def second_layer(i):
+            a, b = OUT_PIECES[i]
+            bank = psum.tile([P, b - a], F32, name="o_bank", tag="bank0%d" % i)
+            nc.tensor.matmul_mx(
+                out=bank[:],
+                lhsT=w2_codes[:].bitcast(FP8X4),
+                lhsT_scale=w2_plane[:],
+                rhs=h_codes[:, a:b].bitcast(FP8X4),
+                rhs_scale=h_plane[:, a:b],
+                start=True,
+                stop=True,
+            )
+            result = keep.tile([P, b - a], F32, name="result%d" % a, align_bytes=64)
+            if i == len(OUT_PIECES) - 1:
+                nc.vector.tensor_copy(result[:], bank[:])
+            else:
+                nc.scalar.copy(result[:], bank[:])
+            nc.sync.dma_start(out[:, a:b], result[:])
+
+        held = add_and_relu(*CHUNKS[0])
+        for c, (a, b) in enumerate(CHUNKS):
+            ahead = add_and_relu(*CHUNKS[c + 1]) if c + 1 < len(CHUNKS) else None
+            quantise_h(a, b, held)
+            held = ahead
+        for i in range(len(OUT_PIECES)):
+            second_layer(i)

@@ -21,7 +21,7 @@ P = 128
 PASSES = 2
 BANK = 512
 POS_PIECES = [(0, 256), (256, 512), (512, 768), (768, 1024)]
-CHUNKS = [(0, 256), (256, 512), (512, 768), (768, 896), (896, 1024)]
+CHUNKS = [(0, 256), (256, 512), (512, 640), (640, 768), (768, 896), (896, 1024)]
 OUT_PIECES = [(0, 512), (512, 768), (768, 896), (896, 1024)]
 M_SPLIT = 84
 
@@ -32,19 +32,20 @@ def tile_picked_phpq_relu_p_kernel(
     nc = tc.nc
     with ExitStack() as ctx:
         keep = ctx.enter_context(tc.tile_pool(name="keep", bufs=1))
+        reuse = ctx.enter_context(tc.tile_pool(name="reuse", bufs=1))
         psum = ctx.enter_context(tc.psum_pool(name="psum", bufs=1))
 
         offsets = keep.tile([P, S // 16], U16, name="offsets")
         nc.sync.dma_start(offsets[:], offs)
 
-        xs_table = keep.tile([P, T], U8, name="xs_table", tag="slot_a", align_bytes=64)
+        xs_table = reuse.tile([P, T], U8, name="xs_table", align_bytes=64, offset=3072)
         nc.gpsimd.memset(xs_table[:].bitcast(I32), 0)
-        nc.scalar.dma_start(
+        nc.sync.dma_start(
             xs_table[0:P:4, :].bitcast(I32), x_scales.bitcast(I32).rearrange("z q c -> q z c")
         )
 
-        def load_x(z, tag):
-            table = keep.tile([P, T], U32, name="xw_table%d" % z, tag=tag, align_bytes=64)
+        def load_x(z):
+            table = keep.tile([P, T], U32, name="xw_table%d" % z, align_bytes=64)
             nc.sync.dma_start(table[:].bitcast(I32), x_words[z].rearrange("p n t -> p (n t)").bitcast(I32))
             return table
 
@@ -52,11 +53,14 @@ def tile_picked_phpq_relu_p_kernel(
             rows = w1[512 * z : 512 * (z + 1), 256 * u : 256 * (u + 1)]
             nc.sync.dma_start(raw, rows.rearrange("(p j) c -> p j c", j=4))
 
-        xw_table0 = load_x(0, "slot_b")
+        xw_table0 = load_x(0)
         w0a = keep.tile([P, 4, 256], F32, name="w0a", align_bytes=64)
         w0b = keep.tile([P, 4, 256], F32, name="w0b", tag="slot_c", align_bytes=64)
         load_w(0, 0, w0a[:])
         load_w(0, 1, w0b[:])
+        xw_table1 = load_x(1)
+        w1a = keep.tile([P, 4, 256], F32, name="w1a", align_bytes=64)
+        load_w(1, 0, w1a[:])
 
         xs_plane = keep.tile([P, PASSES * S], U8, name="xs_plane", align_bytes=64)
         nc.vector.memset(xs_plane[:].bitcast(I32), 0)
@@ -76,25 +80,19 @@ def tile_picked_phpq_relu_p_kernel(
                 xs_plane[32 * q : 32 * q + 4, :].bitcast(I32),
                 xs_picked[32 * q : 32 * q + 32 : 4, :].bitcast(I32),
             )
-        xw_table1 = load_x(1, "slot_a")
 
-        def gather_words(z, table):
-            picked = keep.tile([P, S], U32, name="xw_picked%d" % z, align_bytes=64)
-            nc.vector.tensor_copy(picked[:], table[:].indirect(offsets[:]))
-            return picked
+        w1b = reuse.tile([P, 4, 256], F32, name="w1b", align_bytes=64, offset=4096)
+        load_w(1, 1, w1b[:])
+        xw_picked0 = reuse.tile([P, S], U32, name="xw_picked0", align_bytes=64, offset=0)
+        nc.vector.tensor_copy(xw_picked0[:], xw_table0[:].indirect(offsets[:]))
 
-        xw_picked = [gather_words(0, xw_table0)]
-        w1ab = keep.tile([P, 2, 4, 256], F32, name="w1ab", tag="slot_b", align_bytes=64)
-        load_w(1, 0, w1ab[:, 0])
-        load_w(1, 1, w1ab[:, 1])
-
-        grouped = [keep.tile([P, 4, 128, 4], BF16, name="w_grouped%d" % z, align_bytes=64) for z in range(PASSES)]
+        grouped = [keep.tile([P, 4, 128, 4], BF16, name="w_grouped%d" % z, tag="slot_g%d" % z, align_bytes=64) for z in range(PASSES)]
         w_codes = [keep.tile([P, H], U32, name="w_codes%d" % z, align_bytes=64) for z in range(PASSES)]
         w_plane = [keep.tile([P, H], U8, name="w_plane%d" % z, align_bytes=64) for z in range(PASSES)]
 
         def cast_views(z, raw, base, m0, m1):
-            dst = grouped[z][:, :, m0:m1, :].rearrange("p t m j -> p m j t")
-            src = raw[:, :, 4 * (m0 - base) : 4 * (m1 - base)].rearrange("p j (m t) -> p m j t", t=4)
+            dst = grouped[z][:, :, m0:m1, :].rearrange("p t m j -> p m t j")
+            src = raw[:, :, 4 * (m0 - base) : 4 * (m1 - base)].rearrange("p j (m t) -> p m t j", t=4)
             return dst, src
 
         def quantise_w(z, t0, t1):
@@ -114,41 +112,47 @@ def tile_picked_phpq_relu_p_kernel(
         for a, b in POS_PIECES:
             nc.sync.dma_start(pos_sb[:, :, a:b], pos_view[:, :, a:b])
 
-        banks = [[psum.tile([P, BANK], F32, name="h_bank", tag="bank%d%d" % (g, t)) for t in range(4)] for g in range(2)]
+        wide = [psum.tile([P, BANK], F32, name="wide", tag="bank%d" % t) for t in range(4)]
+        narrow = [psum.tile([P, 4, 128], F32, name="narrow", tag="bank%d" % (4 + c)) for c in range(4)]
 
-        def first_layer(z):
-            for g in range(2):
-                for t in range(4):
-                    m_cols = slice(128 * t, 128 * (t + 1))
-                    nc.tensor.matmul_mx(
-                        out=banks[g][t][:],
-                        lhsT=w_codes[z][:, m_cols].bitcast(FP8X4),
-                        lhsT_scale=w_plane[z][:, m_cols],
-                        rhs=xw_picked[z][:, g * BANK : (g + 1) * BANK].bitcast(FP8X4),
-                        rhs_scale=xs_plane[:, z * S + g * BANK : z * S + (g + 1) * BANK],
-                        start=(z == 0),
-                        stop=(z == PASSES - 1),
-                    )
+        def first_layer(z, t, a, b, dst):
+            m_cols = slice(128 * t, 128 * (t + 1))
+            nc.tensor.matmul_mx(
+                out=dst,
+                lhsT=w_codes[z][:, m_cols].bitcast(FP8X4),
+                lhsT_scale=w_plane[z][:, m_cols],
+                rhs=xw_picked[z][:, a:b].bitcast(FP8X4),
+                rhs_scale=xs_plane[:, z * S + a : z * S + b],
+                start=(z == 0),
+                stop=(z == PASSES - 1),
+            )
 
-        first_layer(0)
-        xw_picked.append(gather_words(1, xw_table1))
-        nc.scalar.activation(*cast_views(1, w1ab[:, 0], 0, 0, 64), COPY)
-        nc.scalar.activation(*cast_views(1, w1ab[:, 1], 64, 64, M_SPLIT), COPY)
-        nc.vector.tensor_copy(*cast_views(1, w1ab[:, 1], 64, M_SPLIT, 128))
+        xw_picked1 = keep.tile([P, S], U32, name="xw_picked1", tag="slot_g0", align_bytes=64)
+        xw_picked = [xw_picked0, xw_picked1]
+        for t in range(4):
+            first_layer(0, t, 0, BANK, wide[t][:])
+        nc.vector.tensor_copy(xw_picked1[:], xw_table1[:].indirect(offsets[:]))
+        nc.scalar.activation(*cast_views(1, w1a[:], 0, 0, 64), COPY)
+        nc.scalar.activation(*cast_views(1, w1b[:], 64, 64, 128), COPY)
         for t in range(4):
             quantise_w(1, t, t + 1)
-        first_layer(1)
+        for t in range(4):
+            first_layer(1, t, 0, BANK, wide[t][:])
+        for c in range(4):
+            for t in range(4):
+                for z in range(PASSES):
+                    first_layer(z, t, BANK + 128 * c, BANK + 128 * (c + 1), narrow[c][:, t, :])
 
         h_codes = keep.tile([P, S], U32, name="h_codes", align_bytes=64)
         h_plane = keep.tile([P, S], U8, name="h_plane", align_bytes=64)
 
         def add_and_relu(a, b):
-            g = a // BANK
             summed = keep.tile([P, 4, b - a], F32, name="summed%d" % a, align_bytes=64)
-            for t in range(4):
-                nc.vector.tensor_tensor(
-                    summed[:, t, :], banks[g][t][:, a - g * BANK : b - g * BANK], pos_sb[:, t, a:b], ADD
-                )
+            if a < BANK:
+                for t in range(4):
+                    nc.vector.tensor_tensor(summed[:, t, :], wide[t][:, a:b], pos_sb[:, t, a:b], ADD)
+            else:
+                nc.vector.tensor_tensor(summed[:], narrow[(a - BANK) // 128][:], pos_sb[:, :, a:b], ADD)
             h_bf = keep.tile([P, b - a, 4], BF16, name="h_bf%d" % a, align_bytes=64)
             dst = h_bf[:].rearrange("p (c i) t -> p c t i", i=4)
             src = summed[:].rearrange("p t (c i) -> p c t i", i=4)
@@ -165,7 +169,7 @@ def tile_picked_phpq_relu_p_kernel(
 
         def second_layer(i):
             a, b = OUT_PIECES[i]
-            bank = psum.tile([P, b - a], F32, name="o_bank", tag="bank0%d" % i)
+            bank = psum.tile([P, b - a], F32, name="o_bank", tag="bank%d" % i)
             nc.tensor.matmul_mx(
                 out=bank[:],
                 lhsT=w2_codes[:].bitcast(FP8X4),
@@ -187,5 +191,6 @@ def tile_picked_phpq_relu_p_kernel(
             ahead = add_and_relu(*CHUNKS[c + 1]) if c + 1 < len(CHUNKS) else None
             quantise_h(a, b, held)
             held = ahead
-        for i in range(len(OUT_PIECES)):
-            second_layer(i)
+            for i, piece in enumerate(OUT_PIECES):
+                if piece[1] == b:
+                    second_layer(i)

@@ -20,10 +20,8 @@ RELU = mybir.ActivationFunctionType.Relu
 P = 128
 PASSES = 2
 BANK = 512
-POS_PIECES = [(0, 256), (256, 512), (512, 768), (768, 1024)]
-CHUNKS = [(0, 256), (256, 512), (512, 640), (640, 768), (768, 896), (896, 1024)]
+POS_PIECES = [(0, 4, 0, 256), (0, 4, 256, 512), (0, 4, 512, 768), (0, 4, 768, 1024)]
 OUT_PIECES = [(0, 512), (512, 768), (768, 896), (896, 1024)]
-M_SPLIT = 84
 
 
 def tile_picked_phpq_relu_p_kernel(
@@ -45,22 +43,16 @@ def tile_picked_phpq_relu_p_kernel(
         )
 
         def load_x(z):
-            table = keep.tile([P, T], U32, name="xw_table%d" % z, align_bytes=64)
+            table = keep.tile([P, T], U32, name="xw_table%d" % z, tag="slot_x%d" % z, align_bytes=64)
             nc.sync.dma_start(table[:].bitcast(I32), x_words[z].rearrange("p n t -> p (n t)").bitcast(I32))
             return table
 
-        def load_w(z, u, raw):
-            rows = w1[512 * z : 512 * (z + 1), 256 * u : 256 * (u + 1)]
-            nc.sync.dma_start(raw, rows.rearrange("(p j) c -> p j c", j=4))
-
+        w0 = keep.tile([P, 4, H], F32, name="w0", tag="slot_c", align_bytes=64)
+        nc.sync.dma_start(w0[:], w1[0:512, :].rearrange("(p j) c -> p j c", j=4))
         xw_table0 = load_x(0)
-        w0a = keep.tile([P, 4, 256], F32, name="w0a", align_bytes=64)
-        w0b = keep.tile([P, 4, 256], F32, name="w0b", tag="slot_c", align_bytes=64)
-        load_w(0, 0, w0a[:])
-        load_w(0, 1, w0b[:])
         xw_table1 = load_x(1)
         w1a = keep.tile([P, 4, 256], F32, name="w1a", align_bytes=64)
-        load_w(1, 0, w1a[:])
+        nc.sync.dma_start(w1a[:], w1[512:1024, 0:256].rearrange("(p j) c -> p j c", j=4))
 
         xs_plane = keep.tile([P, PASSES * S], U8, name="xs_plane", align_bytes=64)
         nc.vector.memset(xs_plane[:].bitcast(I32), 0)
@@ -82,40 +74,33 @@ def tile_picked_phpq_relu_p_kernel(
             )
 
         w1b = reuse.tile([P, 4, 256], F32, name="w1b", align_bytes=64, offset=4096)
-        load_w(1, 1, w1b[:])
+        nc.sync.dma_start(w1b[:], w1[512:1024, 256:512].rearrange("(p j) c -> p j c", j=4))
         xw_picked0 = reuse.tile([P, S], U32, name="xw_picked0", align_bytes=64, offset=0)
         nc.vector.tensor_copy(xw_picked0[:], xw_table0[:].indirect(offsets[:]))
 
-        grouped = [keep.tile([P, 4, 128, 4], BF16, name="w_grouped%d" % z, tag="slot_g%d" % z, align_bytes=64) for z in range(PASSES)]
+        grouped0 = keep.tile([P, 4, 128, 4], BF16, name="w_grouped0", tag="slot_g0", align_bytes=64)
         w_codes = [keep.tile([P, H], U32, name="w_codes%d" % z, align_bytes=64) for z in range(PASSES)]
         w_plane = [keep.tile([P, H], U8, name="w_plane%d" % z, align_bytes=64) for z in range(PASSES)]
 
-        def cast_views(z, raw, base, m0, m1):
-            dst = grouped[z][:, :, m0:m1, :].rearrange("p t m j -> p m t j")
-            src = raw[:, :, 4 * (m0 - base) : 4 * (m1 - base)].rearrange("p j (m t) -> p m t j", t=4)
-            return dst, src
+        def cast_views(dst, raw, m0, m1):
+            src = raw[:, :, 4 * m0 : 4 * m1].rearrange("p j (m t) -> p m t j", t=4)
+            return dst.rearrange("p t m j -> p m t j"), src
 
-        def quantise_w(z, t0, t1):
-            cols = slice(128 * t0, 128 * t1)
-            nc.vector.quantize_mx(
-                out=w_codes[z][:, cols].bitcast(FP8X4),
-                scales=w_plane[z][:, cols],
-                in_=grouped[z][:, t0:t1].rearrange("p t m j -> p (t m j)"),
-            )
+        def quantise_w(z, a, b, grouped):
+            nc.vector.quantize_mx(out=w_codes[z][:, a:b].bitcast(FP8X4), scales=w_plane[z][:, a:b], in_=grouped)
 
-        nc.scalar.activation(*cast_views(0, w0a[:], 0, 0, 64), COPY)
-        nc.scalar.activation(*cast_views(0, w0b[:], 64, 64, 128), COPY)
-        quantise_w(0, 0, 4)
+        nc.scalar.activation(*cast_views(grouped0[:], w0[:], 0, 128), COPY)
+        quantise_w(0, 0, H, grouped0[:].rearrange("p t m j -> p (t m j)"))
 
         pos_view = pos.rearrange("(p t) j -> p t j", t=4)
         pos_sb = keep.tile([P, 4, S], F32, name="pos_sb", tag="slot_c", align_bytes=64)
-        for a, b in POS_PIECES:
-            nc.sync.dma_start(pos_sb[:, :, a:b], pos_view[:, :, a:b])
+        for t0, t1, a, b in POS_PIECES:
+            nc.sync.dma_start(pos_sb[:, t0:t1, a:b], pos_view[:, t0:t1, a:b])
 
         wide = [psum.tile([P, BANK], F32, name="wide", tag="bank%d" % t) for t in range(4)]
-        narrow = [psum.tile([P, 4, 128], F32, name="narrow", tag="bank%d" % (4 + c)) for c in range(4)]
+        narrow = [psum.tile([P, 2, 256], F32, name="narrow", tag="bank%d" % (4 + c)) for c in range(4)]
 
-        def first_layer(z, t, a, b, dst):
+        def first_layer(z, t, a, b, dst, opens):
             m_cols = slice(128 * t, 128 * (t + 1))
             nc.tensor.matmul_mx(
                 out=dst,
@@ -123,39 +108,48 @@ def tile_picked_phpq_relu_p_kernel(
                 lhsT_scale=w_plane[z][:, m_cols],
                 rhs=xw_picked[z][:, a:b].bitcast(FP8X4),
                 rhs_scale=xs_plane[:, z * S + a : z * S + b],
-                start=(z == 0),
-                stop=(z == PASSES - 1),
+                start=opens,
+                stop=not opens,
             )
 
         xw_picked1 = keep.tile([P, S], U32, name="xw_picked1", tag="slot_g0", align_bytes=64)
         xw_picked = [xw_picked0, xw_picked1]
         for t in range(4):
-            first_layer(0, t, 0, BANK, wide[t][:])
+            first_layer(0, t, 0, BANK, wide[t][:], True)
         nc.vector.tensor_copy(xw_picked1[:], xw_table1[:].indirect(offsets[:]))
-        nc.scalar.activation(*cast_views(1, w1a[:], 0, 0, 64), COPY)
-        nc.scalar.activation(*cast_views(1, w1b[:], 64, 64, 128), COPY)
+        low = keep.tile([P, 4, 64, 4], BF16, name="w_low", align_bytes=64)
+        high = keep.tile([P, 4, 64, 4], BF16, name="w_high", tag="slot_x1", align_bytes=64)
+        nc.scalar.activation(*cast_views(low[:], w1a[:], 0, 64), COPY)
+        nc.scalar.activation(*cast_views(high[:, :, 0:24], w1b[:], 0, 24), COPY)
+        nc.vector.tensor_copy(*cast_views(high[:, :, 24:64], w1b[:], 24, 64))
         for t in range(4):
-            quantise_w(1, t, t + 1)
+            for u, half in enumerate((low, high)):
+                quantise_w(1, 128 * t + 64 * u, 128 * t + 64 * (u + 1), half[:, t].rearrange("p m j -> p (m j)"))
         for t in range(4):
-            first_layer(1, t, 0, BANK, wide[t][:])
-        for c in range(4):
+            first_layer(1, t, 0, BANK, wide[t][:], False)
+        for c in range(2):
             for t in range(4):
-                for z in range(PASSES):
-                    first_layer(z, t, BANK + 128 * c, BANK + 128 * (c + 1), narrow[c][:, t, :])
+                for z in (1, 0):
+                    first_layer(z, t, BANK + 256 * c, BANK + 256 * (c + 1), narrow[2 * c + t // 2][:, t % 2, :], z == 1)
 
         h_codes = keep.tile([P, S], U32, name="h_codes", align_bytes=64)
         h_plane = keep.tile([P, S], U8, name="h_plane", align_bytes=64)
 
-        def add_and_relu(a, b):
+        def add_pos(a, b):
             summed = keep.tile([P, 4, b - a], F32, name="summed%d" % a, align_bytes=64)
             if a < BANK:
                 for t in range(4):
                     nc.vector.tensor_tensor(summed[:, t, :], wide[t][:, a:b], pos_sb[:, t, a:b], ADD)
             else:
-                nc.vector.tensor_tensor(summed[:], narrow[(a - BANK) // 128][:], pos_sb[:, :, a:b], ADD)
+                for u in range(2):
+                    pair = slice(2 * u, 2 * u + 2)
+                    nc.vector.tensor_tensor(summed[:, pair, :], narrow[(a - BANK) // 128 + u][:], pos_sb[:, pair, a:b], ADD)
+            return summed
+
+        def relu(summed, a, b):
             h_bf = keep.tile([P, b - a, 4], BF16, name="h_bf%d" % a, align_bytes=64)
             dst = h_bf[:].rearrange("p (c i) t -> p c t i", i=4)
-            src = summed[:].rearrange("p t (c i) -> p c t i", i=4)
+            src = summed.rearrange("p t (c i) -> p c t i", i=4)
             if b == S:
                 nc.vector.tensor_scalar_max(dst, src, 0.0)
             else:
@@ -180,17 +174,24 @@ def tile_picked_phpq_relu_p_kernel(
                 stop=True,
             )
             result = keep.tile([P, b - a], F32, name="result%d" % a, align_bytes=64)
-            if i == len(OUT_PIECES) - 1:
+            if i == 2:
                 nc.vector.tensor_copy(result[:], bank[:])
             else:
                 nc.scalar.copy(result[:], bank[:])
             nc.sync.dma_start(out[:, a:b], result[:])
 
-        held = add_and_relu(*CHUNKS[0])
-        for c, (a, b) in enumerate(CHUNKS):
-            ahead = add_and_relu(*CHUNKS[c + 1]) if c + 1 < len(CHUNKS) else None
-            quantise_h(a, b, held)
-            held = ahead
-            for i, piece in enumerate(OUT_PIECES):
-                if piece[1] == b:
-                    second_layer(i)
+        h0 = relu(add_pos(0, 256)[:], 0, 256)
+        h1 = relu(add_pos(256, 512)[:], 256, 512)
+        quantise_h(0, 256, h0)
+        h2 = relu(add_pos(512, 768)[:], 512, 768)
+        quantise_h(256, 512, h1)
+        second_layer(0)
+        last = add_pos(768, 1024)
+        h3 = relu(last[:, :, 0:128], 768, 896)
+        h4 = relu(last[:, :, 128:256], 896, 1024)
+        quantise_h(512, 768, h2)
+        second_layer(1)
+        quantise_h(896, 1024, h4)
+        second_layer(3)
+        quantise_h(768, 896, h3)
+        second_layer(2)

@@ -13,14 +13,15 @@ U16 = mybir.dt.uint16
 U8 = mybir.dt.uint8
 FP8X4 = mybir.dt.float8_e4m3fn_x4
 ADD = mybir.AluOpType.add
-MAX = mybir.AluOpType.max
 COPY = mybir.ActivationFunctionType.Copy
 RELU = mybir.ActivationFunctionType.Relu
 
 P = 128
 PASSES = 2
 BANK = 512
-POS_PIECES = [(0, 4, 0, 256), (0, 4, 256, 512), (0, 4, 512, 768), (0, 4, 768, 1024)]
+X_FIRST = 512
+SCALAR_M = (64, 44)
+POS_PIECES = [(0, 512), (512, 1024)]
 OUT_PIECES = [(0, 512), (512, 768), (768, 896), (896, 1024)]
 
 
@@ -30,40 +31,38 @@ def tile_picked_phpq_relu_p_kernel(
     nc = tc.nc
     with ExitStack() as ctx:
         keep = ctx.enter_context(tc.tile_pool(name="keep", bufs=1))
-        reuse = ctx.enter_context(tc.tile_pool(name="reuse", bufs=1))
+        after_scales = ctx.enter_context(tc.tile_pool(name="after_scales", bufs=1))
+        after_cast = ctx.enter_context(tc.tile_pool(name="after_cast", bufs=1))
         psum = ctx.enter_context(tc.psum_pool(name="psum", bufs=1))
 
         offsets = keep.tile([P, S // 16], U16, name="offsets")
         nc.sync.dma_start(offsets[:], offs)
 
-        xs_table = reuse.tile([P, T], U8, name="xs_table", align_bytes=64, offset=3072)
-        nc.gpsimd.memset(xs_table[:].bitcast(I32), 0)
+        def load_x(z, table, a, b):
+            words = x_words[z].rearrange("p n t -> p (n t)").bitcast(I32)
+            nc.sync.dma_start(table[:, a:b].bitcast(I32), words[:, a:b])
+
+        xw_table0 = keep.tile([P, T], U32, name="xw_table0", align_bytes=64)
+        load_x(0, xw_table0, 0, X_FIRST)
+
+        xs_table = after_scales.tile([P, T], U8, name="xs_table", align_bytes=64, offset=0)
+        nc.vector.memset(xs_table[:].bitcast(I32), 0)
         nc.sync.dma_start(
             xs_table[0:P:4, :].bitcast(I32), x_scales.bitcast(I32).rearrange("z q c -> q z c")
         )
 
-        def load_x(z):
-            table = keep.tile([P, T], U32, name="xw_table%d" % z, tag="slot_x%d" % z, align_bytes=64)
-            nc.sync.dma_start(table[:].bitcast(I32), x_words[z].rearrange("p n t -> p (n t)").bitcast(I32))
-            return table
 
-        w0 = keep.tile([P, 4, H], F32, name="w0", tag="slot_c", align_bytes=64)
-        nc.sync.dma_start(w0[:], w1[0:512, :].rearrange("(p j) c -> p j c", j=4))
-        xw_table0 = load_x(0)
-        xw_table1 = load_x(1)
-        w1a = keep.tile([P, 4, 256], F32, name="w1a", align_bytes=64)
-        nc.sync.dma_start(w1a[:], w1[512:1024, 0:256].rearrange("(p j) c -> p j c", j=4))
+        def load_w(z, raw):
+            nc.sync.dma_start(raw[:], w1[512 * z : 512 * (z + 1), :].rearrange("(p j) c -> p j c", j=4))
+
+        load_x(0, xw_table0, X_FIRST, T)
+        w_raw0 = after_cast.tile([P, 4, H], F32, name="w_raw0", align_bytes=64, offset=0)
+        load_w(0, w_raw0)
+        xw_table1 = keep.tile([P, T], U32, name="xw_table1", align_bytes=64)
+        load_x(1, xw_table1, 0, T)
 
         xs_plane = keep.tile([P, PASSES * S], U8, name="xs_plane", align_bytes=64)
         nc.vector.memset(xs_plane[:].bitcast(I32), 0)
-        w2_codes = keep.tile([P, N], U32, name="w2_codes", align_bytes=64)
-        w2_plane = keep.tile([P, N], U8, name="w2_plane", align_bytes=64)
-        nc.vector.memset(w2_plane[:].bitcast(I32), 0)
-        nc.gpsimd.dma_start(w2_codes[:].bitcast(I32), w2_words[0].rearrange("p n t -> p (n t)").bitcast(I32))
-        for q in range(4):
-            nc.gpsimd.dma_start(
-                w2_plane[32 * q : 32 * q + 4, :].bitcast(I32), w2_scales[0, 4 * q : 4 * q + 4, :].bitcast(I32)
-            )
 
         xs_picked = keep.tile([P, S], U8, name="xs_picked", align_bytes=64)
         nc.vector.tensor_copy(xs_picked[:], xs_table[:].indirect(offsets[:]))
@@ -73,64 +72,73 @@ def tile_picked_phpq_relu_p_kernel(
                 xs_picked[32 * q : 32 * q + 32 : 4, :].bitcast(I32),
             )
 
-        w1b = reuse.tile([P, 4, 256], F32, name="w1b", align_bytes=64, offset=4096)
-        nc.sync.dma_start(w1b[:], w1[512:1024, 256:512].rearrange("(p j) c -> p j c", j=4))
-        xw_picked0 = reuse.tile([P, S], U32, name="xw_picked0", align_bytes=64, offset=0)
+        w_raw1 = after_scales.tile([P, 4, H], F32, name="w_raw1", align_bytes=64, offset=0)
+        load_w(1, w_raw1)
+        xw_picked0 = keep.tile([P, S], U32, name="xw_picked0", align_bytes=64)
         nc.vector.tensor_copy(xw_picked0[:], xw_table0[:].indirect(offsets[:]))
 
-        grouped0 = keep.tile([P, 4, 128, 4], BF16, name="w_grouped0", tag="slot_g0", align_bytes=64)
         w_codes = [keep.tile([P, H], U32, name="w_codes%d" % z, align_bytes=64) for z in range(PASSES)]
         w_plane = [keep.tile([P, H], U8, name="w_plane%d" % z, align_bytes=64) for z in range(PASSES)]
 
-        def cast_views(dst, raw, m0, m1):
-            src = raw[:, :, 4 * m0 : 4 * m1].rearrange("p j (m t) -> p m t j", t=4)
-            return dst.rearrange("p t m j -> p m t j"), src
+        def cast_views(grouped, raw, m0, m1):
+            src = raw[:, :, 4 * m0 : 4 * m1].rearrange("p j (m t) -> p m j t", t=4)
+            return grouped[:, :, m0:m1].rearrange("p t m j -> p m j t"), src
+
+        def cast_w(z, grouped, raw):
+            nc.scalar.activation(*cast_views(grouped, raw, 0, SCALAR_M[z]), COPY)
+            nc.vector.tensor_copy(*cast_views(grouped, raw, SCALAR_M[z], P))
 
         def quantise_w(z, a, b, grouped):
             nc.vector.quantize_mx(out=w_codes[z][:, a:b].bitcast(FP8X4), scales=w_plane[z][:, a:b], in_=grouped)
 
-        nc.scalar.activation(*cast_views(grouped0[:], w0[:], 0, 128), COPY)
+        grouped0 = keep.tile([P, 4, P, 4], BF16, name="w_grouped0", align_bytes=64)
+        cast_w(0, grouped0, w_raw0)
+
         quantise_w(0, 0, H, grouped0[:].rearrange("p t m j -> p (t m j)"))
 
         pos_view = pos.rearrange("(p t) j -> p t j", t=4)
-        pos_sb = keep.tile([P, 4, S], F32, name="pos_sb", tag="slot_c", align_bytes=64)
-        for t0, t1, a, b in POS_PIECES:
-            nc.sync.dma_start(pos_sb[:, t0:t1, a:b], pos_view[:, t0:t1, a:b])
+        pos_sb = after_cast.tile([P, 4, S], F32, name="pos_sb", align_bytes=64, offset=5120)
+        for a, b in POS_PIECES:
+            nc.sync.dma_start(pos_sb[:, :, a:b], pos_view[:, :, a:b])
+        w2_codes = after_cast.tile([P, N], U32, name="w2_codes", align_bytes=64, offset=4096)
+        nc.sync.dma_start(w2_codes[:].bitcast(I32), w2_words[0].rearrange("p n t -> p (n t)").bitcast(I32))
+        w2_plane = after_cast.tile([P, N], U8, name="w2_plane", align_bytes=64, offset=4608)
+        nc.gpsimd.memset(w2_plane[:].bitcast(I32), 0)
+        for q in range(4):
+            nc.sync.dma_start(
+                w2_plane[32 * q : 32 * q + 4, :].bitcast(I32), w2_scales[0, 4 * q : 4 * q + 4, :].bitcast(I32)
+            )
+
 
         wide = [psum.tile([P, BANK], F32, name="wide", tag="bank%d" % t) for t in range(4)]
         narrow = [psum.tile([P, 2, 256], F32, name="narrow", tag="bank%d" % (4 + c)) for c in range(4)]
 
-        def first_layer(z, t, a, b, dst, opens):
-            m_cols = slice(128 * t, 128 * (t + 1))
+        def first_layer(z, picked, t, a, b, dst, opens):
+            m_cols = slice(P * t, P * (t + 1))
             nc.tensor.matmul_mx(
                 out=dst,
                 lhsT=w_codes[z][:, m_cols].bitcast(FP8X4),
                 lhsT_scale=w_plane[z][:, m_cols],
-                rhs=xw_picked[z][:, a:b].bitcast(FP8X4),
+                rhs=picked[:, a:b].bitcast(FP8X4),
                 rhs_scale=xs_plane[:, z * S + a : z * S + b],
                 start=opens,
                 stop=not opens,
             )
 
-        xw_picked1 = keep.tile([P, S], U32, name="xw_picked1", tag="slot_g0", align_bytes=64)
-        xw_picked = [xw_picked0, xw_picked1]
         for t in range(4):
-            first_layer(0, t, 0, BANK, wide[t][:], True)
+            first_layer(0, xw_picked0, t, 0, BANK, wide[t][:], True)
+        xw_picked1 = after_cast.tile([P, S], U32, name="xw_picked1", align_bytes=64, offset=0)
         nc.vector.tensor_copy(xw_picked1[:], xw_table1[:].indirect(offsets[:]))
-        low = keep.tile([P, 4, 64, 4], BF16, name="w_low", align_bytes=64)
-        high = keep.tile([P, 4, 64, 4], BF16, name="w_high", tag="slot_x1", align_bytes=64)
-        nc.scalar.activation(*cast_views(low[:], w1a[:], 0, 64), COPY)
-        nc.scalar.activation(*cast_views(high[:, :, 0:24], w1b[:], 0, 24), COPY)
-        nc.vector.tensor_copy(*cast_views(high[:, :, 24:64], w1b[:], 24, 64))
+        grouped1 = keep.tile([P, 4, P, 4], BF16, name="w_grouped1", align_bytes=64)
+        cast_w(1, grouped1, w_raw1)
         for t in range(4):
-            for u, half in enumerate((low, high)):
-                quantise_w(1, 128 * t + 64 * u, 128 * t + 64 * (u + 1), half[:, t].rearrange("p m j -> p (m j)"))
+            quantise_w(1, P * t, P * (t + 1), grouped1[:, t].rearrange("p m j -> p (m j)"))
         for t in range(4):
-            first_layer(1, t, 0, BANK, wide[t][:], False)
+            first_layer(1, xw_picked1, t, 0, BANK, wide[t][:], False)
         for c in range(2):
             for t in range(4):
-                for z in (1, 0):
-                    first_layer(z, t, BANK + 256 * c, BANK + 256 * (c + 1), narrow[2 * c + t // 2][:, t % 2, :], z == 1)
+                for z, picked in ((1, xw_picked1), (0, xw_picked0)):
+                    first_layer(z, picked, t, BANK + 256 * c, BANK + 256 * (c + 1), narrow[2 * c + t // 2][:, t % 2, :], z == 1)
 
         h_codes = keep.tile([P, S], U32, name="h_codes", align_bytes=64)
         h_plane = keep.tile([P, S], U8, name="h_plane", align_bytes=64)
@@ -144,7 +152,7 @@ def tile_picked_phpq_relu_p_kernel(
                 for u in range(2):
                     pair = slice(2 * u, 2 * u + 2)
                     nc.vector.tensor_tensor(summed[:, pair, :], narrow[(a - BANK) // 128 + u][:], pos_sb[:, pair, a:b], ADD)
-            return summed
+            return summed[:]
 
         def relu(summed, a, b):
             h_bf = keep.tile([P, b - a, 4], BF16, name="h_bf%d" % a, align_bytes=64)
@@ -180,10 +188,10 @@ def tile_picked_phpq_relu_p_kernel(
                 nc.scalar.copy(result[:], bank[:])
             nc.sync.dma_start(out[:, a:b], result[:])
 
-        h0 = relu(add_pos(0, 256)[:], 0, 256)
-        h1 = relu(add_pos(256, 512)[:], 256, 512)
+        h0 = relu(add_pos(0, 256), 0, 256)
+        h1 = relu(add_pos(256, 512), 256, 512)
         quantise_h(0, 256, h0)
-        h2 = relu(add_pos(512, 768)[:], 512, 768)
+        h2 = relu(add_pos(512, 768), 512, 768)
         quantise_h(256, 512, h1)
         second_layer(0)
         last = add_pos(768, 1024)

@@ -18,10 +18,9 @@ RELU = mybir.ActivationFunctionType.Relu
 
 P = 128
 PASSES = 2
-BANK = 512
 X_FIRST = 512
 SCALAR_M = (64, 44)
-POS_PIECES = [(0, 512), (512, 1024)]
+POS_PIECES = [(0, 256), (256, 512), (512, 768), (768, 1024)]
 OUT_PIECES = [(0, 512), (512, 768), (768, 896), (896, 1024)]
 
 
@@ -110,8 +109,7 @@ def tile_picked_phpq_relu_p_kernel(
             )
 
 
-        wide = [psum.tile([P, BANK], F32, name="wide", tag="bank%d" % t) for t in range(4)]
-        narrow = [psum.tile([P, 2, 256], F32, name="narrow", tag="bank%d" % (4 + c)) for c in range(4)]
+        banks = [psum.tile([P, 2, 256], F32, name="z", tag="bank%d" % i) for i in range(8)]
 
         def first_layer(z, picked, t, a, b, dst, opens):
             m_cols = slice(P * t, P * (t + 1))
@@ -125,33 +123,31 @@ def tile_picked_phpq_relu_p_kernel(
                 stop=not opens,
             )
 
-        for t in range(4):
-            first_layer(0, xw_picked0, t, 0, BANK, wide[t][:], True)
+        for c in range(4):
+            for u in range(2):
+                first_layer(0, xw_picked0, 2 * u, 256 * c, 256 * (c + 1), banks[2 * c + u][:, 0, :], True)
         xw_picked1 = after_cast.tile([P, S], U32, name="xw_picked1", align_bytes=64, offset=0)
         nc.vector.tensor_copy(xw_picked1[:], xw_table1[:].indirect(offsets[:]))
         grouped1 = keep.tile([P, 4, P, 4], BF16, name="w_grouped1", align_bytes=64)
         cast_w(1, grouped1, w_raw1)
         for t in range(4):
             quantise_w(1, P * t, P * (t + 1), grouped1[:, t].rearrange("p m j -> p (m j)"))
-        for t in range(4):
-            first_layer(1, xw_picked1, t, 0, BANK, wide[t][:], False)
-        for c in range(2):
-            for t in range(4):
-                for z, picked in ((1, xw_picked1), (0, xw_picked0)):
-                    first_layer(z, picked, t, BANK + 256 * c, BANK + 256 * (c + 1), narrow[2 * c + t // 2][:, t % 2, :], z == 1)
+        for c in range(4):
+            for u in range(2):
+                a, b, bank = 256 * c, 256 * (c + 1), banks[2 * c + u]
+                first_layer(1, xw_picked1, 2 * u, a, b, bank[:, 0, :], False)
+                first_layer(0, xw_picked0, 2 * u + 1, a, b, bank[:, 1, :], True)
+                first_layer(1, xw_picked1, 2 * u + 1, a, b, bank[:, 1, :], False)
 
         h_codes = keep.tile([P, S], U32, name="h_codes", align_bytes=64)
+        result = keep.tile([P, S], F32, name="result", align_bytes=64)
         h_plane = keep.tile([P, S], U8, name="h_plane", align_bytes=64)
 
         def add_pos(a, b):
             summed = keep.tile([P, 4, b - a], F32, name="summed%d" % a, align_bytes=64)
-            if a < BANK:
-                for t in range(4):
-                    nc.vector.tensor_tensor(summed[:, t, :], wide[t][:, a:b], pos_sb[:, t, a:b], ADD)
-            else:
-                for u in range(2):
-                    pair = slice(2 * u, 2 * u + 2)
-                    nc.vector.tensor_tensor(summed[:, pair, :], narrow[(a - BANK) // 128 + u][:], pos_sb[:, pair, a:b], ADD)
+            for u in range(2):
+                pair = slice(2 * u, 2 * u + 2)
+                nc.vector.tensor_tensor(summed[:, pair, :], banks[a // 128 + u][:], pos_sb[:, pair, a:b], ADD)
             return summed[:]
 
         def relu(summed, a, b):
@@ -181,12 +177,13 @@ def tile_picked_phpq_relu_p_kernel(
                 start=True,
                 stop=True,
             )
-            result = keep.tile([P, b - a], F32, name="result%d" % a, align_bytes=64)
             if i == 2:
-                nc.vector.tensor_copy(result[:], bank[:])
+                nc.vector.tensor_copy(result[:, a:b], bank[:])
+                nc.sync.dma_start(out[:, a:S], result[:, a:S])
             else:
-                nc.scalar.copy(result[:], bank[:])
-            nc.sync.dma_start(out[:, a:b], result[:])
+                nc.scalar.copy(result[:, a:b], bank[:])
+                if b < S:
+                    nc.sync.dma_start(out[:, a:b], result[:, a:b])
 
         h0 = relu(add_pos(0, 256), 0, 256)
         h1 = relu(add_pos(256, 512), 256, 512)

@@ -20,8 +20,7 @@ P = 128
 PASSES = 2
 X_FIRST = 512
 SCALAR_M = (64, 44)
-POS_PIECES = [(0, 256), (256, 512), (512, 768), (768, 1024)]
-OUT_PIECES = [(0, 512), (512, 768), (768, 896), (896, 1024)]
+POS_PIECES = [(0, 2, 0, 512), (2, 4, 0, 512), (0, 1, 512, 1024), (1, 2, 512, 1024), (2, 3, 512, 1024), (3, 4, 512, 1024)]
 
 
 def tile_picked_phpq_relu_p_kernel(
@@ -32,6 +31,7 @@ def tile_picked_phpq_relu_p_kernel(
         keep = ctx.enter_context(tc.tile_pool(name="keep", bufs=1))
         after_scales = ctx.enter_context(tc.tile_pool(name="after_scales", bufs=1))
         after_cast = ctx.enter_context(tc.tile_pool(name="after_cast", bufs=1))
+        after_adds = ctx.enter_context(tc.tile_pool(name="after_adds", bufs=1))
         psum = ctx.enter_context(tc.psum_pool(name="psum", bufs=1))
 
         offsets = keep.tile([P, S // 16], U16, name="offsets")
@@ -97,8 +97,8 @@ def tile_picked_phpq_relu_p_kernel(
 
         pos_view = pos.rearrange("(p t) j -> p t j", t=4)
         pos_sb = after_cast.tile([P, 4, S], F32, name="pos_sb", align_bytes=64, offset=5120)
-        for a, b in POS_PIECES:
-            nc.sync.dma_start(pos_sb[:, :, a:b], pos_view[:, :, a:b])
+        for t0, t1, a, b in POS_PIECES:
+            nc.sync.dma_start(pos_sb[:, t0:t1, a:b], pos_view[:, t0:t1, a:b])
         w2_codes = after_cast.tile([P, N], U32, name="w2_codes", align_bytes=64, offset=4096)
         nc.sync.dma_start(w2_codes[:].bitcast(I32), w2_words[0].rearrange("p n t -> p (n t)").bitcast(I32))
         w2_plane = after_cast.tile([P, N], U8, name="w2_plane", align_bytes=64, offset=4608)
@@ -108,8 +108,8 @@ def tile_picked_phpq_relu_p_kernel(
                 w2_plane[32 * q : 32 * q + 4, :].bitcast(I32), w2_scales[0, 4 * q : 4 * q + 4, :].bitcast(I32)
             )
 
-
-        banks = [psum.tile([P, 2, 256], F32, name="z", tag="bank%d" % i) for i in range(8)]
+        narrow = [psum.tile([P, 2, 256], F32, name="z_narrow", tag="bank%d" % i) for i in range(4)]
+        wide = [psum.tile([P, 512], F32, name="z_wide", tag="bank%d" % (4 + t)) for t in range(4)]
 
         def first_layer(z, picked, t, a, b, dst, opens):
             m_cols = slice(P * t, P * (t + 1))
@@ -123,80 +123,104 @@ def tile_picked_phpq_relu_p_kernel(
                 stop=not opens,
             )
 
-        for c in range(4):
+        for c in range(2):
             for u in range(2):
-                first_layer(0, xw_picked0, 2 * u, 256 * c, 256 * (c + 1), banks[2 * c + u][:, 0, :], True)
+                first_layer(0, xw_picked0, 2 * u, 256 * c, 256 * (c + 1), narrow[2 * c + u][:, 0, :], True)
+        for t in range(2):
+            first_layer(0, xw_picked0, t, 512, S, wide[t][:], True)
         xw_picked1 = after_cast.tile([P, S], U32, name="xw_picked1", align_bytes=64, offset=0)
         nc.vector.tensor_copy(xw_picked1[:], xw_table1[:].indirect(offsets[:]))
         grouped1 = keep.tile([P, 4, P, 4], BF16, name="w_grouped1", align_bytes=64)
         cast_w(1, grouped1, w_raw1)
         for t in range(4):
             quantise_w(1, P * t, P * (t + 1), grouped1[:, t].rearrange("p m j -> p (m j)"))
-        for c in range(4):
-            for u in range(2):
-                a, b, bank = 256 * c, 256 * (c + 1), banks[2 * c + u]
-                first_layer(1, xw_picked1, 2 * u, a, b, bank[:, 0, :], False)
-                first_layer(0, xw_picked0, 2 * u + 1, a, b, bank[:, 1, :], True)
-                first_layer(1, xw_picked1, 2 * u + 1, a, b, bank[:, 1, :], False)
 
-        h_codes = keep.tile([P, S], U32, name="h_codes", align_bytes=64)
+        def close_narrow(c, u):
+            a, b, bank = 256 * c, 256 * (c + 1), narrow[2 * c + u]
+            first_layer(1, xw_picked1, 2 * u, a, b, bank[:, 0, :], False)
+            first_layer(0, xw_picked0, 2 * u + 1, a, b, bank[:, 1, :], True)
+            first_layer(1, xw_picked1, 2 * u + 1, a, b, bank[:, 1, :], False)
+
+        def close_wide(t):
+            first_layer(1, xw_picked1, t, 512, S, wide[t][:], False)
+
+        def late_wide(t):
+            first_layer(1, xw_picked1, t, 512, S, wide[t][:], True)
+            first_layer(0, xw_picked0, t, 512, S, wide[t][:], False)
+
+        close_wide(0)
+        close_narrow(0, 0)
+        close_narrow(0, 1)
+        close_wide(1)
+        close_narrow(1, 0)
+        close_narrow(1, 1)
+        late_wide(2)
+        late_wide(3)
+
         result = keep.tile([P, S], F32, name="result", align_bytes=64)
         h_plane = keep.tile([P, S], U8, name="h_plane", align_bytes=64)
+        summed = [keep.tile([P, 4, 512], F32, name="summed%d" % h, align_bytes=64) for h in range(2)]
+        h_bf = [keep.tile([P, 256, 4], BF16, name="h_bf%d" % c, align_bytes=64) for c in range(4)]
 
-        def add_pos(a, b):
-            summed = keep.tile([P, 4, b - a], F32, name="summed%d" % a, align_bytes=64)
+        def add_narrow(c):
+            cols = slice(256 * c, 256 * (c + 1))
             for u in range(2):
                 pair = slice(2 * u, 2 * u + 2)
-                nc.vector.tensor_tensor(summed[:, pair, :], banks[a // 128 + u][:], pos_sb[:, pair, a:b], ADD)
-            return summed[:]
+                nc.vector.tensor_tensor(summed[0][:, pair, cols], narrow[2 * c + u][:], pos_sb[:, pair, cols], ADD)
 
-        def relu(summed, a, b):
-            h_bf = keep.tile([P, b - a, 4], BF16, name="h_bf%d" % a, align_bytes=64)
-            dst = h_bf[:].rearrange("p (c i) t -> p c t i", i=4)
-            src = summed.rearrange("p t (c i) -> p c t i", i=4)
-            if b == S:
-                nc.vector.tensor_scalar_max(dst, src, 0.0)
-            else:
-                nc.scalar.activation(dst, src, RELU)
-            return h_bf
+        def add_wide(t, a, b):
+            nc.vector.tensor_tensor(summed[1][:, t, a:b], wide[t][:, a:b], pos_sb[:, t, 512 + a : 512 + b], ADD)
 
-        def quantise_h(a, b, h_bf):
+        def add_on_gpsimd(t):
+            z_sb = after_adds.tile([P, 512], F32, name="z_sb%d" % t, align_bytes=64, offset=2048 * t)
+            nc.scalar.copy(z_sb[:], wide[t][:])
+            nc.gpsimd.tensor_tensor(summed[1][:, t, :], z_sb[:], pos_sb[:, t, 512:S], ADD)
+
+        def relu_views(rounded, sums):
+            return rounded.rearrange("p (c i) t -> p c t i", i=4), sums.rearrange("p t (c i) -> p c t i", i=4)
+
+        def second_layer(c):
+            cols = slice(256 * c, 256 * (c + 1))
             nc.vector.quantize_mx(
-                out=h_codes[:, a:b].bitcast(FP8X4), scales=h_plane[:, a:b], in_=h_bf[:].rearrange("p n t -> p (n t)")
+                out=h_codes[:, cols].bitcast(FP8X4), scales=h_plane[:, cols], in_=h_bf[c][:].rearrange("p n t -> p (n t)")
             )
-
-        def second_layer(i):
-            a, b = OUT_PIECES[i]
-            bank = psum.tile([P, b - a], F32, name="o_bank", tag="bank%d" % i)
+            bank = psum.tile([P, 256], F32, name="o_bank", tag="bank%d" % c)
             nc.tensor.matmul_mx(
                 out=bank[:],
                 lhsT=w2_codes[:].bitcast(FP8X4),
                 lhsT_scale=w2_plane[:],
-                rhs=h_codes[:, a:b].bitcast(FP8X4),
-                rhs_scale=h_plane[:, a:b],
+                rhs=h_codes[:, cols].bitcast(FP8X4),
+                rhs_scale=h_plane[:, cols],
                 start=True,
                 stop=True,
             )
-            if i == 2:
-                nc.vector.tensor_copy(result[:, a:b], bank[:])
-                nc.sync.dma_start(out[:, a:S], result[:, a:S])
-            else:
-                nc.scalar.copy(result[:, a:b], bank[:])
-                if b < S:
-                    nc.sync.dma_start(out[:, a:b], result[:, a:b])
+            return bank
 
-        h0 = relu(add_pos(0, 256), 0, 256)
-        h1 = relu(add_pos(256, 512), 256, 512)
-        quantise_h(0, 256, h0)
-        h2 = relu(add_pos(512, 768), 512, 768)
-        quantise_h(256, 512, h1)
-        second_layer(0)
-        last = add_pos(768, 1024)
-        h3 = relu(last[:, :, 0:128], 768, 896)
-        h4 = relu(last[:, :, 128:256], 896, 1024)
-        quantise_h(512, 768, h2)
-        second_layer(1)
-        quantise_h(896, 1024, h4)
-        second_layer(3)
-        quantise_h(768, 896, h3)
-        second_layer(2)
+        def store(c, bank, on_vector):
+            cols = slice(256 * c, 256 * (c + 1))
+            if on_vector:
+                nc.vector.tensor_copy(result[:, cols], bank[:])
+            else:
+                nc.scalar.copy(result[:, cols], bank[:])
+            nc.sync.dma_start(out[:, cols], result[:, cols])
+
+        add_on_gpsimd(0)
+        add_on_gpsimd(1)
+        h_codes = after_adds.tile([P, S], U32, name="h_codes", align_bytes=64, offset=0)
+        add_narrow(0)
+        nc.scalar.activation(*relu_views(h_bf[0][:], summed[0][:, :, 0:256]), RELU)
+        add_narrow(1)
+        nc.scalar.activation(*relu_views(h_bf[1][:], summed[0][:, :, 256:512]), RELU)
+        add_wide(2, 0, 512)
+        add_wide(3, 0, 256)
+        nc.scalar.activation(*relu_views(h_bf[2][:], summed[1][:, :, 0:256]), RELU)
+        add_wide(3, 256, 512)
+        o0 = second_layer(0)
+        nc.vector.tensor_scalar_max(*relu_views(h_bf[3][:], summed[1][:, :, 256:512]), 0.0)
+        o1 = second_layer(1)
+        o3 = second_layer(3)
+        o2 = second_layer(2)
+        store(0, o0, False)
+        store(1, o1, False)
+        store(3, o3, False)
+        store(2, o2, True)

@@ -19,8 +19,11 @@ RELU = mybir.ActivationFunctionType.Relu
 P = 128
 PASSES = 2
 X_FIRST = 512
-SCALAR_M = (64, 44)
-POS_PIECES = [(0, 2, 0, 512), (2, 4, 0, 512), (0, 1, 512, 1024), (1, 2, 512, 1024), (2, 3, 512, 1024), (3, 4, 512, 1024)]
+SCALAR_M0 = 64
+SCALAR_M1 = 84
+VECTOR_ADDS = 128
+SCALAR_RELU = 128
+Q = 256
 
 
 def tile_picked_phpq_relu_p_kernel(
@@ -31,7 +34,7 @@ def tile_picked_phpq_relu_p_kernel(
         keep = ctx.enter_context(tc.tile_pool(name="keep", bufs=1))
         after_scales = ctx.enter_context(tc.tile_pool(name="after_scales", bufs=1))
         after_cast = ctx.enter_context(tc.tile_pool(name="after_cast", bufs=1))
-        after_adds = ctx.enter_context(tc.tile_pool(name="after_adds", bufs=1))
+        after_quantise = ctx.enter_context(tc.tile_pool(name="after_quantise", bufs=1))
         psum = ctx.enter_context(tc.psum_pool(name="psum", bufs=1))
 
         offsets = keep.tile([P, S // 16], U16, name="offsets")
@@ -51,12 +54,13 @@ def tile_picked_phpq_relu_p_kernel(
         )
 
 
-        def load_w(z, raw):
-            nc.sync.dma_start(raw[:], w1[512 * z : 512 * (z + 1), :].rearrange("(p j) c -> p j c", j=4))
+        def load_w(z, raw, a, b):
+            rows = w1[512 * z : 512 * (z + 1), :].rearrange("(p j) c -> p j c", j=4)
+            nc.sync.dma_start(raw[:, :, a:b], rows[:, :, a:b])
 
         load_x(0, xw_table0, X_FIRST, T)
         w_raw0 = after_cast.tile([P, 4, H], F32, name="w_raw0", align_bytes=64, offset=0)
-        load_w(0, w_raw0)
+        load_w(0, w_raw0, 0, H)
         xw_table1 = keep.tile([P, T], U32, name="xw_table1", align_bytes=64)
         load_x(1, xw_table1, 0, T)
 
@@ -72,7 +76,8 @@ def tile_picked_phpq_relu_p_kernel(
             )
 
         w_raw1 = after_scales.tile([P, 4, H], F32, name="w_raw1", align_bytes=64, offset=0)
-        load_w(1, w_raw1)
+        load_w(1, w_raw1, 0, H // 2)
+        load_w(1, w_raw1, H // 2, H)
         xw_picked0 = keep.tile([P, S], U32, name="xw_picked0", align_bytes=64)
         nc.vector.tensor_copy(xw_picked0[:], xw_table0[:].indirect(offsets[:]))
 
@@ -83,22 +88,18 @@ def tile_picked_phpq_relu_p_kernel(
             src = raw[:, :, 4 * m0 : 4 * m1].rearrange("p j (m t) -> p m j t", t=4)
             return grouped[:, :, m0:m1].rearrange("p t m j -> p m j t"), src
 
-        def cast_w(z, grouped, raw):
-            nc.scalar.activation(*cast_views(grouped, raw, 0, SCALAR_M[z]), COPY)
-            nc.vector.tensor_copy(*cast_views(grouped, raw, SCALAR_M[z], P))
-
         def quantise_w(z, a, b, grouped):
             nc.vector.quantize_mx(out=w_codes[z][:, a:b].bitcast(FP8X4), scales=w_plane[z][:, a:b], in_=grouped)
 
         grouped0 = keep.tile([P, 4, P, 4], BF16, name="w_grouped0", align_bytes=64)
-        cast_w(0, grouped0, w_raw0)
-
+        nc.scalar.activation(*cast_views(grouped0, w_raw0, 0, SCALAR_M0), COPY)
+        nc.vector.tensor_copy(*cast_views(grouped0, w_raw0, SCALAR_M0, P))
         quantise_w(0, 0, H, grouped0[:].rearrange("p t m j -> p (t m j)"))
 
         pos_view = pos.rearrange("(p t) j -> p t j", t=4)
         pos_sb = after_cast.tile([P, 4, S], F32, name="pos_sb", align_bytes=64, offset=5120)
-        for t0, t1, a, b in POS_PIECES:
-            nc.sync.dma_start(pos_sb[:, t0:t1, a:b], pos_view[:, t0:t1, a:b])
+        for c in range(4):
+            nc.sync.dma_start(pos_sb[:, :, Q * c : Q * (c + 1)], pos_view[:, :, Q * c : Q * (c + 1)])
         w2_codes = after_cast.tile([P, N], U32, name="w2_codes", align_bytes=64, offset=4096)
         nc.sync.dma_start(w2_codes[:].bitcast(I32), w2_words[0].rearrange("p n t -> p (n t)").bitcast(I32))
         w2_plane = after_cast.tile([P, N], U8, name="w2_plane", align_bytes=64, offset=4608)
@@ -108,119 +109,111 @@ def tile_picked_phpq_relu_p_kernel(
                 w2_plane[32 * q : 32 * q + 4, :].bitcast(I32), w2_scales[0, 4 * q : 4 * q + 4, :].bitcast(I32)
             )
 
-        narrow = [psum.tile([P, 2, 256], F32, name="z_narrow", tag="bank%d" % i) for i in range(4)]
-        wide = [psum.tile([P, 512], F32, name="z_wide", tag="bank%d" % (4 + t)) for t in range(4)]
+        banks = [psum.tile([P, 2, Q], F32, name="z_bank", tag="bank%d" % i) for i in range(8)]
 
-        def first_layer(z, picked, t, a, b, dst, opens):
-            m_cols = slice(P * t, P * (t + 1))
-            nc.tensor.matmul_mx(
-                out=dst,
-                lhsT=w_codes[z][:, m_cols].bitcast(FP8X4),
-                lhsT_scale=w_plane[z][:, m_cols],
-                rhs=picked[:, a:b].bitcast(FP8X4),
-                rhs_scale=xs_plane[:, z * S + a : z * S + b],
-                start=opens,
-                stop=not opens,
-            )
+        picked = [xw_picked0]
 
-        for c in range(2):
-            for u in range(2):
-                first_layer(0, xw_picked0, 2 * u, 256 * c, 256 * (c + 1), narrow[2 * c + u][:, 0, :], True)
-        for t in range(2):
-            first_layer(0, xw_picked0, t, 512, S, wide[t][:], True)
+        def first_layer(z, c, u, opens):
+            for e in range(2):
+                m_cols = slice(P * (2 * u + e), P * (2 * u + e + 1))
+                nc.tensor.matmul_mx(
+                    out=banks[2 * c + u][:, e, :],
+                    lhsT=w_codes[z][:, m_cols].bitcast(FP8X4),
+                    lhsT_scale=w_plane[z][:, m_cols],
+                    rhs=picked[z][:, Q * c : Q * (c + 1)].bitcast(FP8X4),
+                    rhs_scale=xs_plane[:, z * S + Q * c : z * S + Q * (c + 1)],
+                    start=(opens and e == 0),
+                    stop=(not opens and e == 1),
+                )
+
+        bank_order = [(0, 0), (1, 1), (0, 1), (2, 1), (1, 0), (3, 1), (2, 0), (3, 0)]
+        for c, u in bank_order:
+            if c < 3:
+                first_layer(0, c, u, True)
         xw_picked1 = after_cast.tile([P, S], U32, name="xw_picked1", align_bytes=64, offset=0)
         nc.vector.tensor_copy(xw_picked1[:], xw_table1[:].indirect(offsets[:]))
+        picked.append(xw_picked1)
         grouped1 = keep.tile([P, 4, P, 4], BF16, name="w_grouped1", align_bytes=64)
-        cast_w(1, grouped1, w_raw1)
+        nc.scalar.activation(*cast_views(grouped1, w_raw1, 0, P // 2), COPY)
+        nc.scalar.activation(*cast_views(grouped1, w_raw1, P // 2, SCALAR_M1), COPY)
+        nc.vector.tensor_copy(*cast_views(grouped1, w_raw1, SCALAR_M1, P))
         for t in range(4):
             quantise_w(1, P * t, P * (t + 1), grouped1[:, t].rearrange("p m j -> p (m j)"))
 
-        def close_narrow(c, u):
-            a, b, bank = 256 * c, 256 * (c + 1), narrow[2 * c + u]
-            first_layer(1, xw_picked1, 2 * u, a, b, bank[:, 0, :], False)
-            first_layer(0, xw_picked0, 2 * u + 1, a, b, bank[:, 1, :], True)
-            first_layer(1, xw_picked1, 2 * u + 1, a, b, bank[:, 1, :], False)
-
-        def close_wide(t):
-            first_layer(1, xw_picked1, t, 512, S, wide[t][:], False)
-
-        def late_wide(t):
-            first_layer(1, xw_picked1, t, 512, S, wide[t][:], True)
-            first_layer(0, xw_picked0, t, 512, S, wide[t][:], False)
-
-        close_wide(0)
-        close_narrow(0, 0)
-        close_narrow(0, 1)
-        close_wide(1)
-        close_narrow(1, 0)
-        close_narrow(1, 1)
-        late_wide(2)
-        late_wide(3)
+        for c, u in bank_order:
+            first_layer(1, c, u, c == 3)
+            if c == 3:
+                first_layer(0, c, u, False)
 
         result = keep.tile([P, S], F32, name="result", align_bytes=64)
+        h_codes = keep.tile([P, S], U32, name="h_codes", align_bytes=64)
         h_plane = keep.tile([P, S], U8, name="h_plane", align_bytes=64)
-        summed = [keep.tile([P, 4, 512], F32, name="summed%d" % h, align_bytes=64) for h in range(2)]
-        h_bf = [keep.tile([P, 256, 4], BF16, name="h_bf%d" % c, align_bytes=64) for c in range(4)]
+        pairs = [keep.tile([P, 2, Q, 2], BF16, name="pairs%d" % c, align_bytes=64) for c in range(3)]
+        h_bf = [after_quantise.tile([P, Q, 4], BF16, name="h_bf%d" % c, align_bytes=64, offset=2048 * c) for c in range(4)]
 
-        def add_narrow(c):
-            cols = slice(256 * c, 256 * (c + 1))
-            for u in range(2):
-                pair = slice(2 * u, 2 * u + 2)
-                nc.vector.tensor_tensor(summed[0][:, pair, cols], narrow[2 * c + u][:], pos_sb[:, pair, cols], ADD)
+        def add_on_gpsimd(c):
+            z_sb = keep.tile([P, Q - VECTOR_ADDS, 2], F32, name="z_sb%d" % c, align_bytes=64)
+            nc.scalar.copy(z_sb[:], banks[2 * c + 1][:, :, VECTOR_ADDS:Q].rearrange("p e j -> p j e"))
+            pos_part = pos_sb[:, 2:4, Q * c + VECTOR_ADDS : Q * (c + 1)].rearrange("p e j -> p j e")
+            nc.gpsimd.tensor_tensor(pairs[c][:, 1, VECTOR_ADDS:Q, :], z_sb[:], pos_part, ADD)
 
-        def add_wide(t, a, b):
-            nc.vector.tensor_tensor(summed[1][:, t, a:b], wide[t][:, a:b], pos_sb[:, t, 512 + a : 512 + b], ADD)
+        def add_on_vector(c, u, n):
+            nc.vector.tensor_tensor(
+                pairs[c][:, u, 0:n, :].rearrange("p (g i) e -> p g e i", i=4),
+                banks[2 * c + u][:, :, 0:n].rearrange("p e (g i) -> p g e i", i=4),
+                pos_sb[:, 2 * u : 2 * u + 2, Q * c : Q * c + n].rearrange("p e (g i) -> p g e i", i=4),
+                ADD,
+            )
 
-        def add_on_gpsimd(t):
-            z_sb = after_adds.tile([P, 512], F32, name="z_sb%d" % t, align_bytes=64, offset=2048 * t)
-            nc.scalar.copy(z_sb[:], wide[t][:])
-            nc.gpsimd.tensor_tensor(summed[1][:, t, :], z_sb[:], pos_sb[:, t, 512:S], ADD)
+        def relu_views(c, a, b):
+            rounded = h_bf[c][:, a:b, :].rearrange("p j (u e) -> p j u e", e=2)
+            return rounded, pairs[c][:, :, a:b, :].rearrange("p u j e -> p j u e")
 
-        def relu_views(rounded, sums):
-            return rounded.rearrange("p (c i) t -> p c t i", i=4), sums.rearrange("p t (c i) -> p c t i", i=4)
-
-        def second_layer(c):
-            cols = slice(256 * c, 256 * (c + 1))
+        def quantise_h(c):
+            cols = slice(Q * c, Q * (c + 1))
             nc.vector.quantize_mx(
                 out=h_codes[:, cols].bitcast(FP8X4), scales=h_plane[:, cols], in_=h_bf[c][:].rearrange("p n t -> p (n t)")
             )
-            bank = psum.tile([P, 256], F32, name="o_bank", tag="bank%d" % c)
+
+        def second_layer(a, b, tag, on_vector):
+            bank = psum.tile([P, b - a], F32, name="o_bank", tag=tag)
             nc.tensor.matmul_mx(
                 out=bank[:],
                 lhsT=w2_codes[:].bitcast(FP8X4),
                 lhsT_scale=w2_plane[:],
-                rhs=h_codes[:, cols].bitcast(FP8X4),
-                rhs_scale=h_plane[:, cols],
+                rhs=h_codes[:, a:b].bitcast(FP8X4),
+                rhs_scale=h_plane[:, a:b],
                 start=True,
                 stop=True,
             )
-            return bank
-
-        def store(c, bank, on_vector):
-            cols = slice(256 * c, 256 * (c + 1))
             if on_vector:
-                nc.vector.tensor_copy(result[:, cols], bank[:])
+                nc.vector.tensor_copy(result[:, a:b], bank[:])
             else:
-                nc.scalar.copy(result[:, cols], bank[:])
-            nc.sync.dma_start(out[:, cols], result[:, cols])
+                nc.scalar.copy(result[:, a:b], bank[:])
+            nc.sync.dma_start(out[:, a:b], result[:, a:b])
 
-        add_on_gpsimd(0)
         add_on_gpsimd(1)
-        h_codes = after_adds.tile([P, S], U32, name="h_codes", align_bytes=64, offset=0)
-        add_narrow(0)
-        nc.scalar.activation(*relu_views(h_bf[0][:], summed[0][:, :, 0:256]), RELU)
-        add_narrow(1)
-        nc.scalar.activation(*relu_views(h_bf[1][:], summed[0][:, :, 256:512]), RELU)
-        add_wide(2, 0, 512)
-        add_wide(3, 0, 256)
-        nc.scalar.activation(*relu_views(h_bf[2][:], summed[1][:, :, 0:256]), RELU)
-        add_wide(3, 256, 512)
-        o0 = second_layer(0)
-        nc.vector.tensor_scalar_max(*relu_views(h_bf[3][:], summed[1][:, :, 256:512]), 0.0)
-        o1 = second_layer(1)
-        o3 = second_layer(3)
-        o2 = second_layer(2)
-        store(0, o0, False)
-        store(1, o1, False)
-        store(3, o3, False)
-        store(2, o2, True)
+        add_on_gpsimd(2)
+        add_on_vector(0, 0, Q)
+        add_on_vector(0, 1, Q)
+        nc.scalar.activation(*relu_views(0, 0, Q), RELU)
+        add_on_vector(1, 0, Q)
+        add_on_vector(1, 1, VECTOR_ADDS)
+        add_on_vector(2, 0, Q)
+        add_on_vector(2, 1, VECTOR_ADDS)
+        quantise_h(0)
+        pairs.append(after_quantise.tile([P, 2, Q, 2], BF16, name="pairs3", align_bytes=64, offset=0))
+        add_on_gpsimd(3)
+        nc.scalar.activation(*relu_views(1, 0, Q), RELU)
+        nc.scalar.activation(*relu_views(2, 0, SCALAR_RELU), RELU)
+        add_on_vector(3, 0, Q)
+        add_on_vector(3, 1, VECTOR_ADDS)
+        nc.vector.tensor_scalar_max(*relu_views(2, SCALAR_RELU, Q), 0.0)
+        quantise_h(1)
+        nc.vector.tensor_scalar_max(*relu_views(3, 0, Q), 0.0)
+        quantise_h(2)
+        quantise_h(3)
+        second_layer(0, Q, "bank0", False)
+        second_layer(Q, 2 * Q, "bank1", False)
+        second_layer(2 * Q, 3 * Q, "bank2", False)
+        second_layer(3 * Q, S, "bank3", True)

@@ -20,10 +20,10 @@ P = 128
 PASSES = 2
 X_FIRST = 512
 SCALAR_M0 = 64
-SCALAR_M1 = 84
-VECTOR_ADDS = 128
-SCALAR_RELU = 128
+SCALAR_M1 = 44
+SCALAR_RELU = 160
 Q = 256
+EARLY_BANKS = 5
 
 
 def tile_picked_phpq_relu_p_kernel(
@@ -34,7 +34,7 @@ def tile_picked_phpq_relu_p_kernel(
         keep = ctx.enter_context(tc.tile_pool(name="keep", bufs=1))
         after_scales = ctx.enter_context(tc.tile_pool(name="after_scales", bufs=1))
         after_cast = ctx.enter_context(tc.tile_pool(name="after_cast", bufs=1))
-        after_quantise = ctx.enter_context(tc.tile_pool(name="after_quantise", bufs=1))
+        after_adds = ctx.enter_context(tc.tile_pool(name="after_adds", bufs=1))
         psum = ctx.enter_context(tc.psum_pool(name="psum", bufs=1))
 
         offsets = keep.tile([P, S // 16], U16, name="offsets")
@@ -76,8 +76,7 @@ def tile_picked_phpq_relu_p_kernel(
             )
 
         w_raw1 = after_scales.tile([P, 4, H], F32, name="w_raw1", align_bytes=64, offset=0)
-        load_w(1, w_raw1, 0, H // 2)
-        load_w(1, w_raw1, H // 2, H)
+        load_w(1, w_raw1, 0, H)
         xw_picked0 = keep.tile([P, S], U32, name="xw_picked0", align_bytes=64)
         nc.vector.tensor_copy(xw_picked0[:], xw_table0[:].indirect(offsets[:]))
 
@@ -98,8 +97,8 @@ def tile_picked_phpq_relu_p_kernel(
 
         pos_view = pos.rearrange("(p t) j -> p t j", t=4)
         pos_sb = after_cast.tile([P, 4, S], F32, name="pos_sb", align_bytes=64, offset=5120)
-        for c in range(4):
-            nc.sync.dma_start(pos_sb[:, :, Q * c : Q * (c + 1)], pos_view[:, :, Q * c : Q * (c + 1)])
+        for u, a, b in ((0, 0, 2 * Q), (1, 0, 2 * Q), (0, 2 * Q, S), (1, 2 * Q, 3 * Q), (1, 3 * Q, S)):
+            nc.sync.dma_start(pos_sb[:, 2 * u : 2 * u + 2, a:b], pos_view[:, 2 * u : 2 * u + 2, a:b])
         w2_codes = after_cast.tile([P, N], U32, name="w2_codes", align_bytes=64, offset=4096)
         nc.sync.dma_start(w2_codes[:].bitcast(I32), w2_words[0].rearrange("p n t -> p (n t)").bitcast(I32))
         w2_plane = after_cast.tile([P, N], U8, name="w2_plane", align_bytes=64, offset=4608)
@@ -126,48 +125,50 @@ def tile_picked_phpq_relu_p_kernel(
                     stop=(not opens and e == 1),
                 )
 
-        bank_order = [(0, 0), (1, 1), (0, 1), (2, 1), (1, 0), (3, 1), (2, 0), (3, 0)]
-        for c, u in bank_order:
-            if c < 3:
-                first_layer(0, c, u, True)
+        bank_order = [(1, 0), (0, 0), (2, 0), (0, 1), (1, 1), (3, 0), (2, 1), (3, 1)]
+        for c, u in bank_order[:EARLY_BANKS]:
+            first_layer(0, c, u, True)
         xw_picked1 = after_cast.tile([P, S], U32, name="xw_picked1", align_bytes=64, offset=0)
         nc.vector.tensor_copy(xw_picked1[:], xw_table1[:].indirect(offsets[:]))
         picked.append(xw_picked1)
         grouped1 = keep.tile([P, 4, P, 4], BF16, name="w_grouped1", align_bytes=64)
-        nc.scalar.activation(*cast_views(grouped1, w_raw1, 0, P // 2), COPY)
-        nc.scalar.activation(*cast_views(grouped1, w_raw1, P // 2, SCALAR_M1), COPY)
+        nc.scalar.activation(*cast_views(grouped1, w_raw1, 0, SCALAR_M1), COPY)
         nc.vector.tensor_copy(*cast_views(grouped1, w_raw1, SCALAR_M1, P))
         for t in range(4):
             quantise_w(1, P * t, P * (t + 1), grouped1[:, t].rearrange("p m j -> p (m j)"))
 
-        for c, u in bank_order:
-            first_layer(1, c, u, c == 3)
-            if c == 3:
+        for i, (c, u) in enumerate(bank_order):
+            late = i >= EARLY_BANKS
+            first_layer(1, c, u, late)
+            if late:
                 first_layer(0, c, u, False)
 
         result = keep.tile([P, S], F32, name="result", align_bytes=64)
-        h_codes = keep.tile([P, S], U32, name="h_codes", align_bytes=64)
         h_plane = keep.tile([P, S], U8, name="h_plane", align_bytes=64)
-        pairs = [keep.tile([P, 2, Q, 2], BF16, name="pairs%d" % c, align_bytes=64) for c in range(3)]
-        h_bf = [after_quantise.tile([P, Q, 4], BF16, name="h_bf%d" % c, align_bytes=64, offset=2048 * c) for c in range(4)]
+        summed = [keep.tile([P, 4, Q], F32, name="summed%d" % c, align_bytes=64) for c in range(3)]
+        pairs = keep.tile([P, 2, Q, 2], BF16, name="pairs", align_bytes=64)
+        h_bf = [keep.tile([P, Q, 4], BF16, name="h_bf%d" % c, align_bytes=64) for c in range(4)]
 
-        def add_on_gpsimd(c):
-            z_sb = keep.tile([P, Q - VECTOR_ADDS, 2], F32, name="z_sb%d" % c, align_bytes=64)
-            nc.scalar.copy(z_sb[:], banks[2 * c + 1][:, :, VECTOR_ADDS:Q].rearrange("p e j -> p j e"))
-            pos_part = pos_sb[:, 2:4, Q * c + VECTOR_ADDS : Q * (c + 1)].rearrange("p e j -> p j e")
-            nc.gpsimd.tensor_tensor(pairs[c][:, 1, VECTOR_ADDS:Q, :], z_sb[:], pos_part, ADD)
+        def add_on_gpsimd(c, offset):
+            z_sb = after_adds.tile([P, 2, Q], F32, name="z_sb%d" % c, align_bytes=64, offset=offset)
+            nc.scalar.copy(z_sb[:], banks[2 * c][:])
+            nc.gpsimd.tensor_tensor(summed[c][:, 0:2, :], z_sb[:], pos_sb[:, 0:2, Q * c : Q * (c + 1)], ADD)
 
-        def add_on_vector(c, u, n):
+        def add_on_vector(c, u):
+            tiles = slice(2 * u, 2 * u + 2)
+            nc.vector.tensor_tensor(summed[c][:, tiles, :], banks[2 * c + u][:], pos_sb[:, tiles, Q * c : Q * (c + 1)], ADD)
+
+        def add_into_pairs(u):
             nc.vector.tensor_tensor(
-                pairs[c][:, u, 0:n, :].rearrange("p (g i) e -> p g e i", i=4),
-                banks[2 * c + u][:, :, 0:n].rearrange("p e (g i) -> p g e i", i=4),
-                pos_sb[:, 2 * u : 2 * u + 2, Q * c : Q * c + n].rearrange("p e (g i) -> p g e i", i=4),
+                pairs[:, u].rearrange("p (g i) e -> p g e i", i=4),
+                banks[6 + u][:].rearrange("p e (g i) -> p g e i", i=4),
+                pos_sb[:, 2 * u : 2 * u + 2, 3 * Q : S].rearrange("p e (g i) -> p g e i", i=4),
                 ADD,
             )
 
         def relu_views(c, a, b):
-            rounded = h_bf[c][:, a:b, :].rearrange("p j (u e) -> p j u e", e=2)
-            return rounded, pairs[c][:, :, a:b, :].rearrange("p u j e -> p j u e")
+            rounded, sums = h_bf[c][:, a:b, :], summed[c][:, :, a:b]
+            return rounded.rearrange("p (g i) t -> p g t i", i=4), sums.rearrange("p t (g i) -> p g t i", i=4)
 
         def quantise_h(c):
             cols = slice(Q * c, Q * (c + 1))
@@ -192,28 +193,27 @@ def tile_picked_phpq_relu_p_kernel(
                 nc.scalar.copy(result[:, a:b], bank[:])
             nc.sync.dma_start(out[:, a:b], result[:, a:b])
 
-        add_on_gpsimd(1)
-        add_on_gpsimd(2)
-        add_on_vector(0, 0, Q)
-        add_on_vector(0, 1, Q)
+        add_on_gpsimd(1, 0)
+        add_on_gpsimd(2, 2048)
+        h_codes = after_adds.tile([P, S], U32, name="h_codes", align_bytes=64, offset=0)
+        add_on_vector(0, 0)
+        add_on_vector(0, 1)
         nc.scalar.activation(*relu_views(0, 0, Q), RELU)
-        add_on_vector(1, 0, Q)
-        add_on_vector(1, 1, VECTOR_ADDS)
-        add_on_vector(2, 0, Q)
-        add_on_vector(2, 1, VECTOR_ADDS)
-        quantise_h(0)
-        pairs.append(after_quantise.tile([P, 2, Q, 2], BF16, name="pairs3", align_bytes=64, offset=0))
-        add_on_gpsimd(3)
+        add_on_vector(1, 1)
         nc.scalar.activation(*relu_views(1, 0, Q), RELU)
+        add_into_pairs(0)
+        add_on_vector(2, 1)
         nc.scalar.activation(*relu_views(2, 0, SCALAR_RELU), RELU)
-        add_on_vector(3, 0, Q)
-        add_on_vector(3, 1, VECTOR_ADDS)
+        quantise_h(0)
+        add_into_pairs(1)
         nc.vector.tensor_scalar_max(*relu_views(2, SCALAR_RELU, Q), 0.0)
         quantise_h(1)
-        nc.vector.tensor_scalar_max(*relu_views(3, 0, Q), 0.0)
+        nc.vector.tensor_scalar_max(
+            h_bf[3][:].rearrange("p j (u e) -> p j u e", e=2), pairs[:].rearrange("p u j e -> p j u e"), 0.0
+        )
         quantise_h(2)
         quantise_h(3)
-        second_layer(0, Q, "bank0", False)
-        second_layer(Q, 2 * Q, "bank1", False)
-        second_layer(2 * Q, 3 * Q, "bank2", False)
-        second_layer(3 * Q, S, "bank3", True)
+        second_layer(0, Q, "bank2", False)
+        second_layer(Q, 2 * Q, "bank0", False)
+        second_layer(2 * Q, 3 * Q, "bank4", False)
+        second_layer(3 * Q, S, "bank1", True)

@@ -20,8 +20,8 @@ P = 128
 PASSES = 2
 X_FIRST = 512
 SCALAR_M0 = 64
-SCALAR_M1 = 44
-SCALAR_RELU = 160
+SCALAR_M1 = 96
+SCALAR_RELU = 208
 Q = 256
 EARLY_BANKS = 5
 
@@ -35,6 +35,7 @@ def tile_picked_phpq_relu_p_kernel(
         after_scales = ctx.enter_context(tc.tile_pool(name="after_scales", bufs=1))
         after_cast = ctx.enter_context(tc.tile_pool(name="after_cast", bufs=1))
         after_adds = ctx.enter_context(tc.tile_pool(name="after_adds", bufs=1))
+        after_w = ctx.enter_context(tc.tile_pool(name="after_w", bufs=1))
         psum = ctx.enter_context(tc.psum_pool(name="psum", bufs=1))
 
         offsets = keep.tile([P, S // 16], U16, name="offsets")
@@ -110,7 +111,7 @@ def tile_picked_phpq_relu_p_kernel(
 
         banks = [psum.tile([P, 2, Q], F32, name="z_bank", tag="bank%d" % i) for i in range(8)]
 
-        picked = [xw_picked0]
+        picked = {(0, c): xw_picked0[:, Q * c : Q * (c + 1)] for c in range(4)}
 
         def first_layer(z, c, u, opens):
             for e in range(2):
@@ -119,7 +120,7 @@ def tile_picked_phpq_relu_p_kernel(
                     out=banks[2 * c + u][:, e, :],
                     lhsT=w_codes[z][:, m_cols].bitcast(FP8X4),
                     lhsT_scale=w_plane[z][:, m_cols],
-                    rhs=picked[z][:, Q * c : Q * (c + 1)].bitcast(FP8X4),
+                    rhs=picked[z, c].bitcast(FP8X4),
                     rhs_scale=xs_plane[:, z * S + Q * c : z * S + Q * (c + 1)],
                     start=(opens and e == 0),
                     stop=(not opens and e == 1),
@@ -128,14 +129,24 @@ def tile_picked_phpq_relu_p_kernel(
         bank_order = [(1, 0), (0, 0), (2, 0), (0, 1), (1, 1), (3, 0), (2, 1), (3, 1)]
         for c, u in bank_order[:EARLY_BANKS]:
             first_layer(0, c, u, True)
-        xw_picked1 = after_cast.tile([P, S], U32, name="xw_picked1", align_bytes=64, offset=0)
-        nc.vector.tensor_copy(xw_picked1[:], xw_table1[:].indirect(offsets[:]))
-        picked.append(xw_picked1)
-        grouped1 = keep.tile([P, 4, P, 4], BF16, name="w_grouped1", align_bytes=64)
-        nc.scalar.activation(*cast_views(grouped1, w_raw1, 0, SCALAR_M1), COPY)
-        nc.vector.tensor_copy(*cast_views(grouped1, w_raw1, SCALAR_M1, P))
-        for t in range(4):
-            quantise_w(1, P * t, P * (t + 1), grouped1[:, t].rearrange("p m j -> p (m j)"))
+        xw_picked1 = after_cast.tile([P, 3 * Q], U32, name="xw_picked1", align_bytes=64, offset=0)
+        nc.vector.tensor_copy(xw_picked1[:], xw_table1[:].indirect(offsets[:, 0 : 3 * Q // 16]))
+        for c in range(3):
+            picked[1, c] = xw_picked1[:, Q * c : Q * (c + 1)]
+        grouped1 = after_w.tile([P, 4, P, 4], BF16, name="w_grouped1", align_bytes=64, offset=0)
+
+        def pair_views(u, m0, m1):
+            src = w_raw1[:, :, 4 * m0 : 4 * m1].rearrange("p j (m t) -> p m j t", t=4)[:, :, :, 2 * u : 2 * u + 2]
+            return grouped1[:, 2 * u : 2 * u + 2, m0:m1].rearrange("p t m j -> p m j t"), src
+
+        nc.scalar.activation(*pair_views(1, 0, SCALAR_M1), COPY)
+        nc.vector.tensor_copy(*pair_views(0, 0, P))
+        nc.vector.tensor_copy(*pair_views(1, SCALAR_M1, P))
+        for u in range(2):
+            quantise_w(1, 2 * P * u, 2 * P * (u + 1), grouped1[:, 2 * u : 2 * u + 2].rearrange("p t m j -> p (t m j)"))
+        xw_last = after_w.tile([P, Q], U32, name="xw_last", align_bytes=64, offset=0)
+        nc.vector.tensor_copy(xw_last[:], xw_table1[:].indirect(offsets[:, 3 * Q // 16 : S // 16]))
+        picked[1, 3] = xw_last[:]
 
         for i, (c, u) in enumerate(bank_order):
             late = i >= EARLY_BANKS
@@ -149,10 +160,11 @@ def tile_picked_phpq_relu_p_kernel(
         pairs = keep.tile([P, 2, Q, 2], BF16, name="pairs", align_bytes=64)
         h_bf = [keep.tile([P, Q, 4], BF16, name="h_bf%d" % c, align_bytes=64) for c in range(4)]
 
-        def add_on_gpsimd(c, offset):
+        def add_on_gpsimd(c, offset, pieces):
             z_sb = after_adds.tile([P, 2, Q], F32, name="z_sb%d" % c, align_bytes=64, offset=offset)
-            nc.scalar.copy(z_sb[:], banks[2 * c][:])
-            nc.gpsimd.tensor_tensor(summed[c][:, 0:2, :], z_sb[:], pos_sb[:, 0:2, Q * c : Q * (c + 1)], ADD)
+            for tiles in pieces:
+                nc.scalar.copy(z_sb[:, tiles, :], banks[2 * c][:, tiles, :])
+                nc.gpsimd.tensor_tensor(summed[c][:, tiles, :], z_sb[:, tiles, :], pos_sb[:, tiles, Q * c : Q * (c + 1)], ADD)
 
         def add_on_vector(c, u):
             tiles = slice(2 * u, 2 * u + 2)
@@ -193,8 +205,8 @@ def tile_picked_phpq_relu_p_kernel(
                 nc.scalar.copy(result[:, a:b], bank[:])
             nc.sync.dma_start(out[:, a:b], result[:, a:b])
 
-        add_on_gpsimd(1, 0)
-        add_on_gpsimd(2, 2048)
+        add_on_gpsimd(1, 0, [slice(0, 1), slice(1, 2)])
+        add_on_gpsimd(2, 2048, [slice(0, 2)])
         h_codes = after_adds.tile([P, S], U32, name="h_codes", align_bytes=64, offset=0)
         add_on_vector(0, 0)
         add_on_vector(0, 1)
@@ -204,16 +216,16 @@ def tile_picked_phpq_relu_p_kernel(
         add_into_pairs(0)
         add_on_vector(2, 1)
         nc.scalar.activation(*relu_views(2, 0, SCALAR_RELU), RELU)
-        quantise_h(0)
         add_into_pairs(1)
-        nc.vector.tensor_scalar_max(*relu_views(2, SCALAR_RELU, Q), 0.0)
+        quantise_h(0)
         quantise_h(1)
         nc.vector.tensor_scalar_max(
             h_bf[3][:].rearrange("p j (u e) -> p j u e", e=2), pairs[:].rearrange("p u j e -> p j u e"), 0.0
         )
-        quantise_h(2)
+        nc.vector.tensor_scalar_max(*relu_views(2, SCALAR_RELU, Q), 0.0)
         quantise_h(3)
+        quantise_h(2)
         second_layer(0, Q, "bank2", False)
         second_layer(Q, 2 * Q, "bank0", False)
-        second_layer(2 * Q, 3 * Q, "bank4", False)
-        second_layer(3 * Q, S, "bank1", True)
+        second_layer(3 * Q, S, "bank4", False)
+        second_layer(2 * Q, 3 * Q, "bank1", True)

@@ -21,9 +21,9 @@ PASSES = 2
 X_FIRST = 512
 SCALAR_M0 = 64
 SCALAR_M1 = 96
-SCALAR_RELU = 208
+VECTOR_RELU = 64
 Q = 256
-EARLY_BANKS = 5
+EARLY_BANKS = 6
 
 
 def tile_picked_phpq_relu_p_kernel(
@@ -35,7 +35,6 @@ def tile_picked_phpq_relu_p_kernel(
         after_scales = ctx.enter_context(tc.tile_pool(name="after_scales", bufs=1))
         after_cast = ctx.enter_context(tc.tile_pool(name="after_cast", bufs=1))
         after_adds = ctx.enter_context(tc.tile_pool(name="after_adds", bufs=1))
-        after_w = ctx.enter_context(tc.tile_pool(name="after_w", bufs=1))
         psum = ctx.enter_context(tc.psum_pool(name="psum", bufs=1))
 
         offsets = keep.tile([P, S // 16], U16, name="offsets")
@@ -133,7 +132,7 @@ def tile_picked_phpq_relu_p_kernel(
         nc.vector.tensor_copy(xw_picked1[:], xw_table1[:].indirect(offsets[:, 0 : 3 * Q // 16]))
         for c in range(3):
             picked[1, c] = xw_picked1[:, Q * c : Q * (c + 1)]
-        grouped1 = after_w.tile([P, 4, P, 4], BF16, name="w_grouped1", align_bytes=64, offset=0)
+        grouped1 = keep.tile([P, 4, P, 4], BF16, name="w_grouped1", align_bytes=64)
 
         def pair_views(u, m0, m1):
             src = w_raw1[:, :, 4 * m0 : 4 * m1].rearrange("p j (m t) -> p m j t", t=4)[:, :, :, 2 * u : 2 * u + 2]
@@ -144,7 +143,7 @@ def tile_picked_phpq_relu_p_kernel(
         nc.vector.tensor_copy(*pair_views(1, SCALAR_M1, P))
         for u in range(2):
             quantise_w(1, 2 * P * u, 2 * P * (u + 1), grouped1[:, 2 * u : 2 * u + 2].rearrange("p t m j -> p (t m j)"))
-        xw_last = after_w.tile([P, Q], U32, name="xw_last", align_bytes=64, offset=0)
+        xw_last = after_scales.tile([P, Q], U32, name="xw_last", align_bytes=64, offset=0)
         nc.vector.tensor_copy(xw_last[:], xw_table1[:].indirect(offsets[:, 3 * Q // 16 : S // 16]))
         picked[1, 3] = xw_last[:]
 
@@ -182,10 +181,12 @@ def tile_picked_phpq_relu_p_kernel(
             rounded, sums = h_bf[c][:, a:b, :], summed[c][:, :, a:b]
             return rounded.rearrange("p (g i) t -> p g t i", i=4), sums.rearrange("p t (g i) -> p g t i", i=4)
 
-        def quantise_h(c):
-            cols = slice(Q * c, Q * (c + 1))
+        def quantise_h(c, a, b):
+            cols = slice(Q * c + a, Q * c + b)
             nc.vector.quantize_mx(
-                out=h_codes[:, cols].bitcast(FP8X4), scales=h_plane[:, cols], in_=h_bf[c][:].rearrange("p n t -> p (n t)")
+                out=h_codes[:, cols].bitcast(FP8X4),
+                scales=h_plane[:, cols],
+                in_=h_bf[c][:, a:b, :].rearrange("p n t -> p (n t)"),
             )
 
         def second_layer(a, b, tag, on_vector):
@@ -203,6 +204,8 @@ def tile_picked_phpq_relu_p_kernel(
                 nc.vector.tensor_copy(result[:, a:b], bank[:])
             else:
                 nc.scalar.copy(result[:, a:b], bank[:])
+
+        def store(a, b):
             nc.sync.dma_start(out[:, a:b], result[:, a:b])
 
         add_on_gpsimd(1, 0, [slice(0, 1), slice(1, 2)])
@@ -215,17 +218,23 @@ def tile_picked_phpq_relu_p_kernel(
         nc.scalar.activation(*relu_views(1, 0, Q), RELU)
         add_into_pairs(0)
         add_on_vector(2, 1)
-        nc.scalar.activation(*relu_views(2, 0, SCALAR_RELU), RELU)
+        nc.scalar.activation(*relu_views(2, VECTOR_RELU, Q), RELU)
         add_into_pairs(1)
-        quantise_h(0)
-        quantise_h(1)
+        quantise_h(0, 0, Q)
         nc.vector.tensor_scalar_max(
             h_bf[3][:].rearrange("p j (u e) -> p j u e", e=2), pairs[:].rearrange("p u j e -> p j u e"), 0.0
         )
-        nc.vector.tensor_scalar_max(*relu_views(2, SCALAR_RELU, Q), 0.0)
-        quantise_h(3)
-        quantise_h(2)
+        quantise_h(1, 0, Q)
+        nc.vector.tensor_scalar_max(*relu_views(2, 0, VECTOR_RELU), 0.0)
+        quantise_h(3, 0, Q)
+        quantise_h(2, 0, Q // 2)
+        quantise_h(2, Q // 2, Q)
         second_layer(0, Q, "bank2", False)
+        store(0, Q)
         second_layer(Q, 2 * Q, "bank0", False)
+        store(Q, 2 * Q)
         second_layer(3 * Q, S, "bank4", False)
-        second_layer(2 * Q, 3 * Q, "bank1", True)
+        store(3 * Q, S)
+        second_layer(2 * Q, 2 * Q + Q // 2, "bank1", True)
+        second_layer(2 * Q + Q // 2, 3 * Q, "bank3", True)
+        store(2 * Q, 3 * Q)

@@ -165,9 +165,11 @@ def tile_picked_phpq_relu_p_kernel(
                 nc.scalar.copy(z_sb[:, tiles, :], banks[2 * c][:, tiles, :])
                 nc.gpsimd.tensor_tensor(summed[c][:, tiles, :], z_sb[:, tiles, :], pos_sb[:, tiles, Q * c : Q * (c + 1)], ADD)
 
-        def add_on_vector(c, u):
+        def add_on_vector(c, u, a, b):
             tiles = slice(2 * u, 2 * u + 2)
-            nc.vector.tensor_tensor(summed[c][:, tiles, :], banks[2 * c + u][:], pos_sb[:, tiles, Q * c : Q * (c + 1)], ADD)
+            nc.vector.tensor_tensor(
+                summed[c][:, tiles, a:b], banks[2 * c + u][:, :, a:b], pos_sb[:, tiles, Q * c + a : Q * c + b], ADD
+            )
 
         def add_into_pairs(u):
             nc.vector.tensor_tensor(
@@ -211,13 +213,14 @@ def tile_picked_phpq_relu_p_kernel(
         add_on_gpsimd(1, 0, [slice(0, 1), slice(1, 2)])
         add_on_gpsimd(2, 2048, [slice(0, 2)])
         h_codes = after_adds.tile([P, S], U32, name="h_codes", align_bytes=64, offset=0)
-        add_on_vector(0, 0)
-        add_on_vector(0, 1)
-        nc.scalar.activation(*relu_views(0, 0, Q), RELU)
-        add_on_vector(1, 1)
+        add_on_vector(0, 0, 0, Q)
+        for a in (0, Q // 2):
+            add_on_vector(0, 1, a, a + Q // 2)
+            nc.scalar.activation(*relu_views(0, a, a + Q // 2), RELU)
+        add_on_vector(1, 1, 0, Q)
         nc.scalar.activation(*relu_views(1, 0, Q), RELU)
         add_into_pairs(0)
-        add_on_vector(2, 1)
+        add_on_vector(2, 1, 0, Q)
         nc.scalar.activation(*relu_views(2, VECTOR_RELU, Q), RELU)
         add_into_pairs(1)
         quantise_h(0, 0, Q)
@@ -225,16 +228,16 @@ def tile_picked_phpq_relu_p_kernel(
             h_bf[3][:].rearrange("p j (u e) -> p j u e", e=2), pairs[:].rearrange("p u j e -> p j u e"), 0.0
         )
         quantise_h(1, 0, Q)
-        nc.vector.tensor_scalar_max(*relu_views(2, 0, VECTOR_RELU), 0.0)
         quantise_h(3, 0, Q)
-        quantise_h(2, 0, Q // 2)
+        nc.vector.tensor_scalar_max(*relu_views(2, 0, VECTOR_RELU), 0.0)
         quantise_h(2, Q // 2, Q)
+        quantise_h(2, 0, Q // 2)
         second_layer(0, Q, "bank2", False)
         store(0, Q)
         second_layer(Q, 2 * Q, "bank0", False)
         store(Q, 2 * Q)
         second_layer(3 * Q, S, "bank4", False)
         store(3 * Q, S)
-        second_layer(2 * Q, 2 * Q + Q // 2, "bank1", True)
-        second_layer(2 * Q + Q // 2, 3 * Q, "bank3", True)
+        second_layer(2 * Q + Q // 2, 3 * Q, "bank1", True)
+        second_layer(2 * Q, 2 * Q + Q // 2, "bank3", True)
         store(2 * Q, 3 * Q)

@@ -18,11 +18,10 @@ RELU = mybir.ActivationFunctionType.Relu
 
 P = 128
 PASSES = 2
+Q = 256
 X_FIRST = 512
 SCALAR_M0 = 64
 SCALAR_M1 = 96
-VECTOR_RELU = 64
-Q = 256
 EARLY_BANKS = 6
 
 
@@ -41,7 +40,7 @@ def tile_picked_phpq_relu_p_kernel(
         nc.sync.dma_start(offsets[:], offs)
 
         def load_x(z, table, a, b):
-            words = x_words[z].rearrange("p n t -> p (n t)").bitcast(I32)
+            words = x_words[z].rearrange("p col j -> p (col j)").bitcast(I32)
             nc.sync.dma_start(table[:, a:b].bitcast(I32), words[:, a:b])
 
         xw_table0 = keep.tile([P, T], U32, name="xw_table0", align_bytes=64)
@@ -50,17 +49,15 @@ def tile_picked_phpq_relu_p_kernel(
         xs_table = after_scales.tile([P, T], U8, name="xs_table", align_bytes=64, offset=0)
         nc.vector.memset(xs_table[:].bitcast(I32), 0)
         nc.sync.dma_start(
-            xs_table[0:P:4, :].bitcast(I32), x_scales.bitcast(I32).rearrange("z q c -> q z c")
+            xs_table[0:P:4, :].bitcast(I32), x_scales.bitcast(I32).rearrange("z row col -> row z col")
         )
 
-
-        def load_w(z, raw, a, b):
-            rows = w1[512 * z : 512 * (z + 1), :].rearrange("(p j) c -> p j c", j=4)
-            nc.sync.dma_start(raw[:, :, a:b], rows[:, :, a:b])
+        def load_w(z, raw):
+            nc.sync.dma_start(raw[:], w1[512 * z : 512 * (z + 1), :].rearrange("(p j) col -> p j col", j=4))
 
         load_x(0, xw_table0, X_FIRST, T)
         w_raw0 = after_cast.tile([P, 4, H], F32, name="w_raw0", align_bytes=64, offset=0)
-        load_w(0, w_raw0, 0, H)
+        load_w(0, w_raw0)
         xw_table1 = keep.tile([P, T], U32, name="xw_table1", align_bytes=64)
         load_x(1, xw_table1, 0, T)
 
@@ -76,31 +73,36 @@ def tile_picked_phpq_relu_p_kernel(
             )
 
         w_raw1 = after_scales.tile([P, 4, H], F32, name="w_raw1", align_bytes=64, offset=0)
-        load_w(1, w_raw1, 0, H)
+        load_w(1, w_raw1)
         xw_picked0 = keep.tile([P, S], U32, name="xw_picked0", align_bytes=64)
         nc.vector.tensor_copy(xw_picked0[:], xw_table0[:].indirect(offsets[:]))
 
         w_codes = [keep.tile([P, H], U32, name="w_codes%d" % z, align_bytes=64) for z in range(PASSES)]
         w_plane = [keep.tile([P, H], U8, name="w_plane%d" % z, align_bytes=64) for z in range(PASSES)]
 
-        def cast_views(grouped, raw, m0, m1):
-            src = raw[:, :, 4 * m0 : 4 * m1].rearrange("p j (m t) -> p m j t", t=4)
-            return grouped[:, :, m0:m1].rearrange("p t m j -> p m j t"), src
+        def cast_views(grouped, raw, t0, t1, m0, m1):
+            src = raw[:, :, 4 * m0 : 4 * m1].rearrange("p j (m t) -> p m j t", t=4)[:, :, :, t0:t1]
+            return grouped[:, t0:t1, m0:m1].rearrange("p t m j -> p m j t"), src
 
-        def quantise_w(z, a, b, grouped):
-            nc.vector.quantize_mx(out=w_codes[z][:, a:b].bitcast(FP8X4), scales=w_plane[z][:, a:b], in_=grouped)
+        def quantise_w(z, grouped, t0, t1):
+            cols = slice(P * t0, P * t1)
+            nc.vector.quantize_mx(
+                out=w_codes[z][:, cols].bitcast(FP8X4),
+                scales=w_plane[z][:, cols],
+                in_=grouped[:, t0:t1].rearrange("p t m j -> p (t m j)"),
+            )
 
         grouped0 = keep.tile([P, 4, P, 4], BF16, name="w_grouped0", align_bytes=64)
-        nc.scalar.activation(*cast_views(grouped0, w_raw0, 0, SCALAR_M0), COPY)
-        nc.vector.tensor_copy(*cast_views(grouped0, w_raw0, SCALAR_M0, P))
-        quantise_w(0, 0, H, grouped0[:].rearrange("p t m j -> p (t m j)"))
+        nc.scalar.activation(*cast_views(grouped0, w_raw0, 0, 4, 0, SCALAR_M0), COPY)
+        nc.vector.tensor_copy(*cast_views(grouped0, w_raw0, 0, 4, SCALAR_M0, P))
+        quantise_w(0, grouped0, 0, 4)
 
-        pos_view = pos.rearrange("(p t) j -> p t j", t=4)
+        pos_view = pos.rearrange("(p t) n -> p t n", t=4)
         pos_sb = after_cast.tile([P, 4, S], F32, name="pos_sb", align_bytes=64, offset=5120)
         for u, a, b in ((0, 0, 2 * Q), (1, 0, 2 * Q), (0, 2 * Q, S), (1, 2 * Q, 3 * Q), (1, 3 * Q, S)):
             nc.sync.dma_start(pos_sb[:, 2 * u : 2 * u + 2, a:b], pos_view[:, 2 * u : 2 * u + 2, a:b])
         w2_codes = after_cast.tile([P, N], U32, name="w2_codes", align_bytes=64, offset=4096)
-        nc.sync.dma_start(w2_codes[:].bitcast(I32), w2_words[0].rearrange("p n t -> p (n t)").bitcast(I32))
+        nc.sync.dma_start(w2_codes[:].bitcast(I32), w2_words[0].rearrange("p col j -> p (col j)").bitcast(I32))
         w2_plane = after_cast.tile([P, N], U8, name="w2_plane", align_bytes=64, offset=4608)
         nc.gpsimd.memset(w2_plane[:].bitcast(I32), 0)
         for q in range(4):
@@ -108,7 +110,7 @@ def tile_picked_phpq_relu_p_kernel(
                 w2_plane[32 * q : 32 * q + 4, :].bitcast(I32), w2_scales[0, 4 * q : 4 * q + 4, :].bitcast(I32)
             )
 
-        banks = [psum.tile([P, 2, Q], F32, name="z_bank", tag="bank%d" % i) for i in range(8)]
+        banks = [psum.tile([P, 2, Q], F32, name="sum_bank", tag="bank%d" % number) for number in range(8)]
 
         picked = {(0, c): xw_picked0[:, Q * c : Q * (c + 1)] for c in range(4)}
 
@@ -133,22 +135,17 @@ def tile_picked_phpq_relu_p_kernel(
         for c in range(3):
             picked[1, c] = xw_picked1[:, Q * c : Q * (c + 1)]
         grouped1 = keep.tile([P, 4, P, 4], BF16, name="w_grouped1", align_bytes=64)
-
-        def pair_views(u, m0, m1):
-            src = w_raw1[:, :, 4 * m0 : 4 * m1].rearrange("p j (m t) -> p m j t", t=4)[:, :, :, 2 * u : 2 * u + 2]
-            return grouped1[:, 2 * u : 2 * u + 2, m0:m1].rearrange("p t m j -> p m j t"), src
-
-        nc.scalar.activation(*pair_views(1, 0, SCALAR_M1), COPY)
-        nc.vector.tensor_copy(*pair_views(0, 0, P))
-        nc.vector.tensor_copy(*pair_views(1, SCALAR_M1, P))
+        nc.scalar.activation(*cast_views(grouped1, w_raw1, 2, 4, 0, SCALAR_M1), COPY)
+        nc.vector.tensor_copy(*cast_views(grouped1, w_raw1, 0, 2, 0, P))
+        nc.vector.tensor_copy(*cast_views(grouped1, w_raw1, 2, 4, SCALAR_M1, P))
         for u in range(2):
-            quantise_w(1, 2 * P * u, 2 * P * (u + 1), grouped1[:, 2 * u : 2 * u + 2].rearrange("p t m j -> p (t m j)"))
+            quantise_w(1, grouped1, 2 * u, 2 * u + 2)
         xw_last = after_scales.tile([P, Q], U32, name="xw_last", align_bytes=64, offset=0)
         nc.vector.tensor_copy(xw_last[:], xw_table1[:].indirect(offsets[:, 3 * Q // 16 : S // 16]))
         picked[1, 3] = xw_last[:]
 
-        for i, (c, u) in enumerate(bank_order):
-            late = i >= EARLY_BANKS
+        for place, (c, u) in enumerate(bank_order):
+            late = place >= EARLY_BANKS
             first_layer(1, c, u, late)
             if late:
                 first_layer(0, c, u, False)
@@ -159,11 +156,11 @@ def tile_picked_phpq_relu_p_kernel(
         pairs = keep.tile([P, 2, Q, 2], BF16, name="pairs", align_bytes=64)
         h_bf = [keep.tile([P, Q, 4], BF16, name="h_bf%d" % c, align_bytes=64) for c in range(4)]
 
-        def add_on_gpsimd(c, offset, pieces):
-            z_sb = after_adds.tile([P, 2, Q], F32, name="z_sb%d" % c, align_bytes=64, offset=offset)
+        def add_on_gpsimd(c, pieces):
+            copied = after_adds.tile([P, 2, Q], F32, name="copied%d" % c, align_bytes=64, offset=2048 * (c - 1))
             for tiles in pieces:
-                nc.scalar.copy(z_sb[:, tiles, :], banks[2 * c][:, tiles, :])
-                nc.gpsimd.tensor_tensor(summed[c][:, tiles, :], z_sb[:, tiles, :], pos_sb[:, tiles, Q * c : Q * (c + 1)], ADD)
+                nc.scalar.copy(copied[:, tiles, :], banks[2 * c][:, tiles, :])
+                nc.gpsimd.tensor_tensor(summed[c][:, tiles, :], copied[:, tiles, :], pos_sb[:, tiles, Q * c : Q * (c + 1)], ADD)
 
         def add_on_vector(c, u, a, b):
             tiles = slice(2 * u, 2 * u + 2)
@@ -173,15 +170,15 @@ def tile_picked_phpq_relu_p_kernel(
 
         def add_into_pairs(u):
             nc.vector.tensor_tensor(
-                pairs[:, u].rearrange("p (g i) e -> p g e i", i=4),
-                banks[6 + u][:].rearrange("p e (g i) -> p g e i", i=4),
-                pos_sb[:, 2 * u : 2 * u + 2, 3 * Q : S].rearrange("p e (g i) -> p g e i", i=4),
+                pairs[:, u].rearrange("p (quad f) e -> p quad e f", f=4),
+                banks[2 * 3 + u][:].rearrange("p e (quad f) -> p quad e f", f=4),
+                pos_sb[:, 2 * u : 2 * u + 2, 3 * Q : S].rearrange("p e (quad f) -> p quad e f", f=4),
                 ADD,
             )
 
         def relu_views(c, a, b):
             rounded, sums = h_bf[c][:, a:b, :], summed[c][:, :, a:b]
-            return rounded.rearrange("p (g i) t -> p g t i", i=4), sums.rearrange("p t (g i) -> p g t i", i=4)
+            return rounded.rearrange("p (quad f) t -> p quad t f", f=4), sums.rearrange("p t (quad f) -> p quad t f", f=4)
 
         def quantise_h(c, a, b):
             cols = slice(Q * c + a, Q * c + b)
@@ -191,8 +188,8 @@ def tile_picked_phpq_relu_p_kernel(
                 in_=h_bf[c][:, a:b, :].rearrange("p n t -> p (n t)"),
             )
 
-        def second_layer(a, b, tag, on_vector):
-            bank = psum.tile([P, b - a], F32, name="o_bank", tag=tag)
+        def second_layer(a, b, bank_number, on_vector):
+            bank = psum.tile([P, b - a], F32, name="o_bank", tag="bank%d" % bank_number)
             nc.tensor.matmul_mx(
                 out=bank[:],
                 lhsT=w2_codes[:].bitcast(FP8X4),
@@ -210,8 +207,8 @@ def tile_picked_phpq_relu_p_kernel(
         def store(a, b):
             nc.sync.dma_start(out[:, a:b], result[:, a:b])
 
-        add_on_gpsimd(1, 0, [slice(0, 1), slice(1, 2)])
-        add_on_gpsimd(2, 2048, [slice(0, 2)])
+        add_on_gpsimd(1, [slice(0, 1), slice(1, 2)])
+        add_on_gpsimd(2, [slice(0, 2)])
         h_codes = after_adds.tile([P, S], U32, name="h_codes", align_bytes=64, offset=0)
         add_on_vector(0, 0, 0, Q)
         for a in (0, Q // 2):
@@ -221,23 +218,23 @@ def tile_picked_phpq_relu_p_kernel(
         nc.scalar.activation(*relu_views(1, 0, Q), RELU)
         add_into_pairs(0)
         add_on_vector(2, 1, 0, Q)
-        nc.scalar.activation(*relu_views(2, VECTOR_RELU, Q), RELU)
+        for a in (Q // 2, 0):
+            nc.scalar.activation(*relu_views(2, a, a + Q // 2), RELU)
         add_into_pairs(1)
         quantise_h(0, 0, Q)
         nc.vector.tensor_scalar_max(
-            h_bf[3][:].rearrange("p j (u e) -> p j u e", e=2), pairs[:].rearrange("p u j e -> p j u e"), 0.0
+            h_bf[3][:].rearrange("p n (u e) -> p n u e", e=2), pairs[:].rearrange("p u n e -> p n u e"), 0.0
         )
         quantise_h(1, 0, Q)
         quantise_h(3, 0, Q)
-        nc.vector.tensor_scalar_max(*relu_views(2, 0, VECTOR_RELU), 0.0)
         quantise_h(2, Q // 2, Q)
         quantise_h(2, 0, Q // 2)
-        second_layer(0, Q, "bank2", False)
+        second_layer(0, Q, 2, False)
         store(0, Q)
-        second_layer(Q, 2 * Q, "bank0", False)
+        second_layer(Q, 2 * Q, 0, False)
         store(Q, 2 * Q)
-        second_layer(3 * Q, S, "bank4", False)
+        second_layer(3 * Q, S, 4, False)
         store(3 * Q, S)
-        second_layer(2 * Q + Q // 2, 3 * Q, "bank1", True)
-        second_layer(2 * Q, 2 * Q + Q // 2, "bank3", True)
+        second_layer(2 * Q + Q // 2, 3 * Q, 1, True)
+        second_layer(2 * Q, 2 * Q + Q // 2, 3, True)
         store(2 * Q, 3 * Q)

@@ -48,9 +48,9 @@ def tile_picked_phpq_relu_p_kernel(
 
         xs_table = after_scales.tile([P, T], U8, name="xs_table", align_bytes=64, offset=0)
         nc.vector.memset(xs_table[:].bitcast(I32), 0)
-        nc.sync.dma_start(
-            xs_table[0:P:4, :].bitcast(I32), x_scales.bitcast(I32).rearrange("z row col -> row z col")
-        )
+        scale_rows = x_scales.bitcast(I32).rearrange("z (g e) col -> e g z col", e=2)
+        for e in range(2):
+            nc.sync.dma_start(xs_table[e:P:8, :].bitcast(I32), scale_rows[e])
 
         def load_w(z, raw):
             nc.sync.dma_start(raw[:], w1[512 * z : 512 * (z + 1), :].rearrange("(p j) col -> p j col", j=4))
@@ -61,16 +61,16 @@ def tile_picked_phpq_relu_p_kernel(
         xw_table1 = keep.tile([P, T], U32, name="xw_table1", align_bytes=64)
         load_x(1, xw_table1, 0, T)
 
-        xs_plane = keep.tile([P, PASSES * S], U8, name="xs_plane", align_bytes=64)
-        nc.vector.memset(xs_plane[:].bitcast(I32), 0)
-
-        xs_picked = keep.tile([P, S], U8, name="xs_picked", align_bytes=64)
+        xs_picked = after_scales.tile([P, S], U8, name="xs_picked", align_bytes=64, offset=2048)
         nc.vector.tensor_copy(xs_picked[:], xs_table[:].indirect(offsets[:]))
-        for q in range(4):
-            nc.sync.dma_start(
-                xs_plane[32 * q : 32 * q + 4, :].bitcast(I32),
-                xs_picked[32 * q : 32 * q + 32 : 4, :].bitcast(I32),
-            )
+        xs_plane = keep.tile([P, S], U8, name="xs_plane", align_bytes=64)
+        nc.vector.tensor_copy(xs_plane[:].bitcast(I32), xs_picked[:].bitcast(I32))
+        for z in range(PASSES):
+            for e in range(2):
+                nc.sync.dma_start(
+                    xs_plane[8 * z + 2 + e : P : 32, :].bitcast(I32),
+                    xs_plane[8 * z + 16 + e : P : 32, :].bitcast(I32),
+                )
 
         w_raw1 = after_scales.tile([P, 4, H], F32, name="w_raw1", align_bytes=64, offset=0)
         load_w(1, w_raw1)
@@ -122,7 +122,7 @@ def tile_picked_phpq_relu_p_kernel(
                     lhsT=w_codes[z][:, m_cols].bitcast(FP8X4),
                     lhsT_scale=w_plane[z][:, m_cols],
                     rhs=picked[z, c].bitcast(FP8X4),
-                    rhs_scale=xs_plane[:, z * S + Q * c : z * S + Q * (c + 1)],
+                    rhs_scale=xs_plane[8 * z : P, Q * c : Q * (c + 1)],
                     start=(opens and e == 0),
                     stop=(not opens and e == 1),
                 )

@@ -20,9 +20,9 @@ P = 128
 PASSES = 2
 Q = 256
 X_FIRST = 512
-SCALAR_M0 = 64
+SCALAR_M0 = 72
 SCALAR_M1 = 96
-EARLY_BANKS = 6
+EARLY_BANKS = 5
 
 
 def tile_picked_phpq_relu_p_kernel(
@@ -62,9 +62,12 @@ def tile_picked_phpq_relu_p_kernel(
         load_x(1, xw_table1, 0, T)
 
         xs_picked = after_scales.tile([P, S], U8, name="xs_picked", align_bytes=64, offset=2048)
-        nc.vector.tensor_copy(xs_picked[:], xs_table[:].indirect(offsets[:]))
+        halves = [slice(0, S // 2), slice(S // 2, S)]
+        for half in halves:
+            nc.vector.tensor_copy(xs_picked[:, half], xs_table[:].indirect(offsets[:, half.start // 16 : half.stop // 16]))
         xs_plane = keep.tile([P, S], U8, name="xs_plane", align_bytes=64)
-        nc.vector.tensor_copy(xs_plane[:].bitcast(I32), xs_picked[:].bitcast(I32))
+        for half in halves:
+            nc.vector.tensor_copy(xs_plane[:, half].bitcast(I32), xs_picked[:, half].bitcast(I32))
         for z in range(PASSES):
             for e in range(2):
                 nc.sync.dma_start(
@@ -233,8 +236,8 @@ def tile_picked_phpq_relu_p_kernel(
         store(0, Q)
         second_layer(Q, 2 * Q, 0, False)
         store(Q, 2 * Q)
-        second_layer(3 * Q, S, 4, False)
+        second_layer(3 * Q, S, 4, True)
         store(3 * Q, S)
-        second_layer(2 * Q + Q // 2, 3 * Q, 1, True)
+        second_layer(2 * Q + Q // 2, 3 * Q, 1, False)
         second_layer(2 * Q, 2 * Q + Q // 2, 3, True)
         store(2 * Q, 3 * Q)

@@ -181,7 +181,7 @@ def tile_picked_phpq_relu_p_kernel(
 
         def relu_views(c, a, b):
             rounded, sums = h_bf[c][:, a:b, :], summed[c][:, :, a:b]
-            return rounded.rearrange("p (quad f) t -> p quad t f", f=4), sums.rearrange("p t (quad f) -> p quad t f", f=4)
+            return rounded.rearrange("p (two f) t -> p two t f", f=2), sums.rearrange("p t (two f) -> p two t f", f=2)
 
         def quantise_h(c, a, b):
             cols = slice(Q * c + a, Q * c + b)

from contextlib import ExitStack

import concourse.mybir as mybir

K, T, S, H, N = 1024, 2048, 1024, 512, 128
FLOPS = 2 * K * H * S + 2 * H * N * S

F32 = mybir.dt.float32
BF16 = mybir.dt.bfloat16
I32 = mybir.dt.int32
U32 = mybir.dt.uint32
U16 = mybir.dt.uint16
U8 = mybir.dt.uint8
FP8X4 = mybir.dt.float8_e4m3fn_x4
ADD = mybir.AluOpType.add
COPY = mybir.ActivationFunctionType.Copy
RELU = mybir.ActivationFunctionType.Relu

P = 128
PASSES = 2
Q = 256
X_FIRST = 512
SCALAR_M0 = 72
SCALAR_M1 = 96
EARLY_BANKS = 5


def tile_picked_phpq_relu_p_kernel(
    tc, x_words, x_scales, w1, w2_words, w2_scales, pos, offs, out
):
    nc = tc.nc
    with ExitStack() as ctx:
        keep = ctx.enter_context(tc.tile_pool(name="keep", bufs=1))
        after_scales = ctx.enter_context(tc.tile_pool(name="after_scales", bufs=1))
        after_cast = ctx.enter_context(tc.tile_pool(name="after_cast", bufs=1))
        after_adds = ctx.enter_context(tc.tile_pool(name="after_adds", bufs=1))
        psum = ctx.enter_context(tc.psum_pool(name="psum", bufs=1))

        offsets = keep.tile([P, S // 16], U16, name="offsets")
        nc.sync.dma_start(offsets[:], offs)

        def load_x(z, table, a, b):
            words = x_words[z].rearrange("p col j -> p (col j)").bitcast(I32)
            nc.sync.dma_start(table[:, a:b].bitcast(I32), words[:, a:b])

        xw_table0 = keep.tile([P, T], U32, name="xw_table0", align_bytes=64)
        load_x(0, xw_table0, 0, X_FIRST)

        xs_table = after_scales.tile([P, T], U8, name="xs_table", align_bytes=64, offset=0)
        nc.vector.memset(xs_table[:].bitcast(I32), 0)
        scale_rows = x_scales.bitcast(I32).rearrange("z (g e) col -> e g z col", e=2)
        for e in range(2):
            nc.sync.dma_start(xs_table[e:P:8, :].bitcast(I32), scale_rows[e])

        def load_w(z, raw):
            nc.sync.dma_start(raw[:], w1[512 * z : 512 * (z + 1), :].rearrange("(p j) col -> p j col", j=4))

        load_x(0, xw_table0, X_FIRST, T)
        w_raw0 = after_cast.tile([P, 4, H], F32, name="w_raw0", align_bytes=64, offset=0)
        load_w(0, w_raw0)
        xw_table1 = keep.tile([P, T], U32, name="xw_table1", align_bytes=64)
        load_x(1, xw_table1, 0, T)

        xs_picked = after_scales.tile([P, S], U8, name="xs_picked", align_bytes=64, offset=2048)
        halves = [slice(0, S // 2), slice(S // 2, S)]
        for half in halves:
            nc.vector.tensor_copy(xs_picked[:, half], xs_table[:].indirect(offsets[:, half.start // 16 : half.stop // 16]))
        xs_plane = keep.tile([P, S], U8, name="xs_plane", align_bytes=64)
        for half in halves:
            nc.vector.tensor_copy(xs_plane[:, half].bitcast(I32), xs_picked[:, half].bitcast(I32))
        for z in range(PASSES):
            for e in range(2):
                nc.sync.dma_start(
                    xs_plane[8 * z + 2 + e : P : 32, :].bitcast(I32),
                    xs_plane[8 * z + 16 + e : P : 32, :].bitcast(I32),
                )

        w_raw1 = after_scales.tile([P, 4, H], F32, name="w_raw1", align_bytes=64, offset=0)
        load_w(1, w_raw1)
        xw_picked0 = keep.tile([P, S], U32, name="xw_picked0", align_bytes=64)
        nc.vector.tensor_copy(xw_picked0[:], xw_table0[:].indirect(offsets[:]))

        w_codes = [keep.tile([P, H], U32, name="w_codes%d" % z, align_bytes=64) for z in range(PASSES)]
        w_plane = [keep.tile([P, H], U8, name="w_plane%d" % z, align_bytes=64) for z in range(PASSES)]

        def cast_views(grouped, raw, t0, t1, m0, m1):
            src = raw[:, :, 4 * m0 : 4 * m1].rearrange("p j (m t) -> p m j t", t=4)[:, :, :, t0:t1]
            return grouped[:, t0:t1, m0:m1].rearrange("p t m j -> p m j t"), src

        def quantise_w(z, grouped, t0, t1):
            cols = slice(P * t0, P * t1)
            nc.vector.quantize_mx(
                out=w_codes[z][:, cols].bitcast(FP8X4),
                scales=w_plane[z][:, cols],
                in_=grouped[:, t0:t1].rearrange("p t m j -> p (t m j)"),
            )

        grouped0 = keep.tile([P, 4, P, 4], BF16, name="w_grouped0", align_bytes=64)
        nc.scalar.activation(*cast_views(grouped0, w_raw0, 0, 4, 0, SCALAR_M0), COPY)
        nc.vector.tensor_copy(*cast_views(grouped0, w_raw0, 0, 4, SCALAR_M0, P))
        quantise_w(0, grouped0, 0, 4)

        pos_view = pos.rearrange("(p t) n -> p t n", t=4)
        pos_sb = after_cast.tile([P, 4, S], F32, name="pos_sb", align_bytes=64, offset=5120)
        for u, a, b in ((0, 0, 2 * Q), (1, 0, 2 * Q), (0, 2 * Q, S), (1, 2 * Q, 3 * Q), (1, 3 * Q, S)):
            nc.sync.dma_start(pos_sb[:, 2 * u : 2 * u + 2, a:b], pos_view[:, 2 * u : 2 * u + 2, a:b])
        w2_codes = after_cast.tile([P, N], U32, name="w2_codes", align_bytes=64, offset=4096)
        nc.sync.dma_start(w2_codes[:].bitcast(I32), w2_words[0].rearrange("p col j -> p (col j)").bitcast(I32))
        w2_plane = after_cast.tile([P, N], U8, name="w2_plane", align_bytes=64, offset=4608)
        nc.gpsimd.memset(w2_plane[:].bitcast(I32), 0)
        for q in range(4):
            nc.sync.dma_start(
                w2_plane[32 * q : 32 * q + 4, :].bitcast(I32), w2_scales[0, 4 * q : 4 * q + 4, :].bitcast(I32)
            )

        banks = [psum.tile([P, 2, Q], F32, name="sum_bank", tag="bank%d" % number) for number in range(8)]

        picked = {(0, c): xw_picked0[:, Q * c : Q * (c + 1)] for c in range(4)}

        def first_layer(z, c, u, opens):
            for e in range(2):
                m_cols = slice(P * (2 * u + e), P * (2 * u + e + 1))
                nc.tensor.matmul_mx(
                    out=banks[2 * c + u][:, e, :],
                    lhsT=w_codes[z][:, m_cols].bitcast(FP8X4),
                    lhsT_scale=w_plane[z][:, m_cols],
                    rhs=picked[z, c].bitcast(FP8X4),
                    rhs_scale=xs_plane[8 * z : P, Q * c : Q * (c + 1)],
                    start=(opens and e == 0),
                    stop=(not opens and e == 1),
                )

        bank_order = [(1, 0), (0, 0), (2, 0), (0, 1), (1, 1), (3, 0), (2, 1), (3, 1)]
        for c, u in bank_order[:EARLY_BANKS]:
            first_layer(0, c, u, True)
        xw_picked1 = after_cast.tile([P, 3 * Q], U32, name="xw_picked1", align_bytes=64, offset=0)
        nc.vector.tensor_copy(xw_picked1[:], xw_table1[:].indirect(offsets[:, 0 : 3 * Q // 16]))
        for c in range(3):
            picked[1, c] = xw_picked1[:, Q * c : Q * (c + 1)]
        grouped1 = keep.tile([P, 4, P, 4], BF16, name="w_grouped1", align_bytes=64)
        nc.scalar.activation(*cast_views(grouped1, w_raw1, 2, 4, 0, SCALAR_M1), COPY)
        nc.vector.tensor_copy(*cast_views(grouped1, w_raw1, 0, 2, 0, P))
        nc.vector.tensor_copy(*cast_views(grouped1, w_raw1, 2, 4, SCALAR_M1, P))
        for u in range(2):
            quantise_w(1, grouped1, 2 * u, 2 * u + 2)
        xw_last = after_scales.tile([P, Q], U32, name="xw_last", align_bytes=64, offset=0)
        nc.vector.tensor_copy(xw_last[:], xw_table1[:].indirect(offsets[:, 3 * Q // 16 : S // 16]))
        picked[1, 3] = xw_last[:]

        for place, (c, u) in enumerate(bank_order):
            late = place >= EARLY_BANKS
            first_layer(1, c, u, late)
            if late:
                first_layer(0, c, u, False)

        result = keep.tile([P, S], F32, name="result", align_bytes=64)
        h_plane = keep.tile([P, S], U8, name="h_plane", align_bytes=64)
        summed = [keep.tile([P, 4, Q], F32, name="summed%d" % c, align_bytes=64) for c in range(3)]
        pairs = keep.tile([P, 2, Q, 2], BF16, name="pairs", align_bytes=64)
        h_bf = [keep.tile([P, Q, 4], BF16, name="h_bf%d" % c, align_bytes=64) for c in range(4)]

        def add_on_gpsimd(c, pieces):
            copied = after_adds.tile([P, 2, Q], F32, name="copied%d" % c, align_bytes=64, offset=2048 * (c - 1))
            for tiles in pieces:
                nc.scalar.copy(copied[:, tiles, :], banks[2 * c][:, tiles, :])
                nc.gpsimd.tensor_tensor(summed[c][:, tiles, :], copied[:, tiles, :], pos_sb[:, tiles, Q * c : Q * (c + 1)], ADD)

        def add_on_vector(c, u, a, b):
            tiles = slice(2 * u, 2 * u + 2)
            nc.vector.tensor_tensor(
                summed[c][:, tiles, a:b], banks[2 * c + u][:, :, a:b], pos_sb[:, tiles, Q * c + a : Q * c + b], ADD
            )

        def add_into_pairs(u):
            nc.vector.tensor_tensor(
                pairs[:, u].rearrange("p (quad f) e -> p quad e f", f=4),
                banks[2 * 3 + u][:].rearrange("p e (quad f) -> p quad e f", f=4),
                pos_sb[:, 2 * u : 2 * u + 2, 3 * Q : S].rearrange("p e (quad f) -> p quad e f", f=4),
                ADD,
            )

        def relu_views(c, a, b):
            rounded, sums = h_bf[c][:, a:b, :], summed[c][:, :, a:b]
            return rounded.rearrange("p (two f) t -> p two t f", f=2), sums.rearrange("p t (two f) -> p two t f", f=2)

        def quantise_h(c, a, b):
            cols = slice(Q * c + a, Q * c + b)
            nc.vector.quantize_mx(
                out=h_codes[:, cols].bitcast(FP8X4),
                scales=h_plane[:, cols],
                in_=h_bf[c][:, a:b, :].rearrange("p n t -> p (n t)"),
            )

        def second_layer(a, b, bank_number, on_vector):
            bank = psum.tile([P, b - a], F32, name="o_bank", tag="bank%d" % bank_number)
            nc.tensor.matmul_mx(
                out=bank[:],
                lhsT=w2_codes[:].bitcast(FP8X4),
                lhsT_scale=w2_plane[:],
                rhs=h_codes[:, a:b].bitcast(FP8X4),
                rhs_scale=h_plane[:, a:b],
                start=True,
                stop=True,
            )
            if on_vector:
                nc.vector.tensor_copy(result[:, a:b], bank[:])
            else:
                nc.scalar.copy(result[:, a:b], bank[:])

        def store(a, b):
            nc.sync.dma_start(out[:, a:b], result[:, a:b])

        add_on_gpsimd(1, [slice(0, 1), slice(1, 2)])
        add_on_gpsimd(2, [slice(0, 2)])
        h_codes = after_adds.tile([P, S], U32, name="h_codes", align_bytes=64, offset=0)
        add_on_vector(0, 0, 0, Q)
        for a in (0, Q // 2):
            add_on_vector(0, 1, a, a + Q // 2)
            nc.scalar.activation(*relu_views(0, a, a + Q // 2), RELU)
        add_on_vector(1, 1, 0, Q)
        nc.scalar.activation(*relu_views(1, 0, Q), RELU)
        add_into_pairs(0)
        add_on_vector(2, 1, 0, Q)
        for a in (Q // 2, 0):
            nc.scalar.activation(*relu_views(2, a, a + Q // 2), RELU)
        add_into_pairs(1)
        quantise_h(0, 0, Q)
        nc.vector.tensor_scalar_max(
            h_bf[3][:].rearrange("p n (u e) -> p n u e", e=2), pairs[:].rearrange("p u n e -> p n u e"), 0.0
        )
        quantise_h(1, 0, Q)
        quantise_h(3, 0, Q)
        quantise_h(2, Q // 2, Q)
        quantise_h(2, 0, Q // 2)
        second_layer(0, Q, 2, False)
        store(0, Q)
        second_layer(Q, 2 * Q, 0, False)
        store(Q, 2 * Q)
        second_layer(3 * Q, S, 4, True)
        store(3 * Q, S)
        second_layer(2 * Q + Q // 2, 3 * Q, 1, False)
        second_layer(2 * Q, 2 * Q + Q // 2, 3, True)
        store(2 * Q, 3 * Q)
